import numpy as np, ml_dtypes
CORES = [32,160,288,416,80,208,336,464]
N = 8
T, EL, CAP, CAPP = 4096, 2, 1920, 512
E = N * EL
def entries(a): return a.T.reshape(-1)
def pack(v, P): return np.ascontiguousarray(np.asarray(v, np.int32).reshape(-1, P).T)
def lists(rng, how):
    g, q, h, R, K = CAP // CAPP, CAP % CAPP, E // 4, np.arange(N)[:, None], np.arange(E)
    C = np.zeros((N, E), np.int64); s = rng.integers(1, E, N); S = None
    few = rng.integers(1, CAPP // 4 + 1, (N, h)); t = rng.integers(CAPP // 8, 3 * CAPP // 8 + 1, (N, 3)); t[:, 2] = CAPP - t[:, 0] - t[:, 1]
    if how == "uniform":
        C[:, :h] = np.where(R <= g, CAPP, few); C[:, h:] = rng.integers(0, CAP // (2 * N) + 1, (N, E - h)); S = np.stack([rng.permutation(2 * h)[:3] + 1 for r in range(N)])
    if how == "bands":
        a = np.arange(E) % N; C = CAPP * ((R >= a) & (R <= a + g)); C[a[N:], np.arange(N, E)] = rng.integers(1, CAPP + 1, E - N); s[g:] = N - g + rng.integers(0, g, N - g) - np.arange(N - g)
    if how == "full":
        v = rng.integers(CAPP - q + 1, CAPP, h + 1); C[:, :h] = CAPP; C[:, h:2 * h + 1] = (CAP - v) // N; C[rng.integers(N), h:2 * h + 1] += (CAP - v) % N; s = h + (np.arange(N) + rng.integers(2)) % 2
    if how == "late":
        C[:N - 1, :h] = np.where(R <= g, CAPP, few)[:N - 1]; C[N - 1, h:3 * h] = rng.integers(1, CAPP + 1, 2 * h); s = rng.integers(h, 2 * h + 1, N)
    if how == "mesh":
        ev = np.arange(0, E, 2); P = np.stack([rng.permutation(2 * h) for r in range(N)]); S = 2 * P[:, :3] + 1; S[g] = 2 * rng.permutation(2 * h - 1)[:3] + 2
        C[:, ev] = CAPP; C[g, ev[h:]] = q; C[g, ev + 1] = rng.integers(0, (CAPP - q) // 2 + 1, 2 * h); C[g, 1] = 0
        z, y = g + 1 + int(rng.integers(0, g - 1)), 2 * int(rng.integers(1, 2 * h)) + 1; C[z, (y - 2 * P[z, 3] - 1) % E] = 0; C[z, y] = CAPP
    if how == "thin":
        C = rng.integers(0, CAP // N + 1, (N, E)); C[1] = 1; C[[0, N // 2, N - 1]] = 0
    if S is None: S, t = s[:, None], np.full((N, 1), CAPP)
    D = np.zeros((N, E, E), np.int64); Z = C.copy()
    for j in range(S.shape[1]):
        w = rng.integers(np.maximum(Z - t[:, j + 1:].sum(axis=1)[:, None], 0), np.minimum(Z, t[:, j:j + 1]) + 1); D[R, K, (K + S[:, j:j + 1]) % E] = w; Z -= w
    X = np.stack([rng.permutation(np.concatenate([np.repeat(np.arange(E * E), D[r].reshape(-1)), np.full(T - D[r].sum(), -1)])) for r in range(N)]); c = np.append(rng.permutation(E), -1)
    return {"e1": np.stack([pack(w, 16) for w in c[X // E]]), "e2": np.stack([pack(w, 16) for w in c[np.where(X < 0, -1, X % E)]])}
def blank(d):
    for r in range(0, N, 2):
        u, i = np.unique(entries(d["e1"][r])[::-1], return_index=True); d["x"][r][:, T - 1 - i[u >= 0]] = 0
def setup_inputs(rng):
    return dict({"x": rng.standard_normal((N, 128, T), dtype=np.float32).astype(ml_dtypes.bfloat16)}, **lists(rng, "uniform"))
def setup_inputs_bands(rng):
    d = setup_inputs(rng); d.update(lists(rng, "bands"))
    for k in ("x",): d[k] = (d[k].astype(np.float32) * 1048576.0).astype(d[k].dtype)
    blank(d)
    return d
def setup_inputs_full(rng):
    d = setup_inputs(rng); d.update(lists(rng, "full"))
    for k in ("x",): d[k] = (d[k].astype(np.float32) * (1 / 1024.0)).astype(d[k].dtype)
    blank(d)
    return d
def setup_inputs_late(rng):
    d = setup_inputs(rng); d.update(lists(rng, "late"))
    blank(d)
    return d
def setup_inputs_mesh(rng):
    d = setup_inputs(rng); d.update(lists(rng, "mesh"))
    blank(d)
    return d
def setup_inputs_thin(rng):
    d = setup_inputs(rng); d.update(lists(rng, "thin"))
    blank(d)
    return d
def check_inputs(x):
    bad = []; a, b = x["e1"], x["e2"]
    if min(a.min(), b.min()) < -1 or max(a.max(), b.max()) >= E: bad.append("e1 or e2 out of range")
    if ((a < 0) != (b < 0)).any(): bad.append("-1 stands in one of e1 and e2 alone")
    if ((a == b) & (a >= 0)).any(): bad.append("a token's two choices are one expert")
    if max(int(np.bincount(v[v >= 0], minlength=E).max()) for w in (a, b) for v in w) > CAPP: bad.append("more than CAPP tokens of one rank have one expert as first choice, or as second choice")
    return bad
def places(e):
    o = np.argsort(e, kind="stable"); p = np.empty(len(e), np.int64); p[o] = np.arange(len(e)) - np.searchsorted(e[o], e[o]); return p
def reference(x, e1, e2):
    X = np.concatenate(list(x), axis=1); a, b = [np.concatenate([entries(v) for v in w]) for w in (e1, e2)]
    k = np.nonzero(a >= 0)[0]; p = places(a[k])
    c1 = np.minimum(np.bincount(a[k], minlength=E), CAP)
    f = k[p >= CAP]; u = c1[b[f]] + places(b[f])
    Y = np.zeros((128, E * CAP), x.dtype); m = p < CAP; Y[:, CAP * a[k[m]] + p[m]] = X[:, k[m]]
    n = u < CAP; Y[:, CAP * b[f[n]] + u[n]] = X[:, f[n]]
    return {"y": np.stack([Y[:, EL * CAP * r:EL * CAP * (r + 1)] for r in range(N)])}

@@ -1,0 +1,359 @@
+from concourse.bass import DstId, RemoteDMATransfer
+from concourse.mybir import AluOpType, ActivationFunctionType
+
+N, TK, CAP, NC, NX, ZC = 8, 4096, 1920, 4, 4, 256
+OUT = 2 * CAP
+LQ = OUT // 16
+SL = 256 // NC
+WIN = OUT + 16 * SL + 112
+XQ = TK // NX
+BIG = 8192.0
+VIA_CABLE = ("chip",)
+
+_SB = {
+    "bfloat16": dict(land=ZC + N * TK, ysb=OUT, lo=256, gtm=128, d8=128, idm=128, ob=128, t2=128, kup=128, kum=128,
+                     tz=144, zz=144, ones=256, val=16 * SL, win=WIN, aa=1024, ao=512, of=1024, ovl=NC * 256, ee=512,
+                     bb=512),
+    "int32": dict(e1w=256, e2w=256, ip=144, it=144, dm=128, ibm=256, pm=144, tm=144),
+    "float32": dict(hif=4, trs=SL, lt=128, ar=128, rb=128, wc=3, hcol=4, sf=1024, vf=1024, bcol=4, so=512, c1s=2,
+                    qt=2 * SL, q1=2 * SL, s2=512, uu=4 * SL, dd=2 * SL, tt=2 * SL, ef=2 * SL, mm=2 * SL, ls=LQ,
+                    lin=(NC - 1) * LQ),
+    "uint16": dict(offs=SL, lst=LQ),
+}
+SCRATCH = {k: ("sbuf", [128, n], d) for d, b in _SB.items() for k, n in b.items()}
+SCRATCH.update({k: ("psum", [128, 512], "float32") for k in ("pa0", "pa1", "pb0", "pb1", "pc", "pd", "pe", "pf")})
+SCRATCH.update({"xs": ("dram", [5 * 128, XQ], "bfloat16"), "e1all": ("dram", [N * 128, 32], "int32"),
+                "e2all": ("dram", [N * 128, 32], "int32")})
+SEMAPHORES = (["e1o", "e1f", "e1p", "e2o", "e2f", "e2p", "e1l", "e2l", "xl0", "xl1", "xl2", "xl3", "xa", "xf", "xr0",
+               "xr1", "xr2", "xland", "loc", "ovs", "li1", "li2", "li3", "yst", "ysc"] + ["k%d" % i for i in range(90)])
+KINDS = ("chip", "host", "both")
+
+
+def bits(m):
+    return [1 << i for i in range(16) if m >> i & 1]
+
+
+def kind(topo, a, b):
+    if topo.host(a) == topo.host(b):
+        return "chip"
+    return "host" if topo.chip(a) == topo.chip(b) else "both"
+
+
+def rank_program(g, core, T, topo):
+    op, AF = AluOpType, ActivationFunctionType
+    home = [c for c in T.cores if topo.host(c) == topo.host(core) and topo.chip(c) == topo.chip(core)]
+    if not home:
+        return
+    root = home[0]
+    rk = T.rank_of(root)
+
+    def team(rc):
+        cs = [c for c in range(512) if topo.host(c) == topo.host(rc) and topo.chip(c) == topo.chip(rc)]
+        i = cs.index(rc)
+        cs = cs[i:] + cs[:i]
+        ctl, car = cs[0::2], cs[1::2]
+        d0 = [c for c in car if topo.die(c) == topo.die(rc)]
+        d1 = [c for c in car if topo.die(c) != topo.die(rc)]
+        return ctl, [c for p in zip(d0, d1) for c in p]
+
+    ctl, car = team(root)
+    myrack = topo.rack(topo.host(root))
+    peers = [c for c in T.cores if c != root and topo.rack(topo.host(c)) == myrack]
+    part = [c for c in T.cores if topo.rack(topo.host(c)) != myrack and topo.chip(c) == topo.chip(root)
+            and topo.may_write(root, c)][0]
+    fr = T.rank_of(part)
+    pteam = team(part)
+    peerteam = {c: team(c) for c in peers}
+
+    sem = T.sem
+    low = bits(topo.mask(core, peers[0]))
+    other = [c for c in ctl if c != core][0]
+    high = [b for b in bits(topo.mask(core, other)) if b not in low]
+    locn = [0]
+
+    def tr(dcores, src, dst, rsem, engs):
+        ids = []
+        for c in dcores:
+            rid, pid = topo.addr(c, core)
+            ids.append(DstId(rid=rid, pnc=pid))
+        locn[0] += len(engs)
+        return RemoteDMATransfer(dst_ids=ids, dma_engine_mask=sum(engs), remote_sem=sem[rsem], srcs=[src],
+                                 dsts=[dst] * len(ids))
+
+    def send(*trs):
+        g.remote_dma_fused(list(trs), local_sem=sem.loc)
+
+    def wait(q, *pairs):
+        for s, v in pairs:
+            q.wait_ge(sem[s], v)
+
+    if core in car:
+        q = car.index(core)
+        cols = lambda s: T.land[:, ZC + TK * s + XQ * q:ZC + TK * s + XQ * (q + 1)]
+        slot = lambda k: T.xs[128 * k:128 * (k + 1), :]
+        direct = [c for c in peers if kind(topo, root, c) not in VIA_CABLE]
+        relay = [(c, KINDS.index(kind(topo, root, c))) for c in peers if kind(topo, root, c) in VIA_CABLE]
+        wait(g, ("xa", 8))
+        send(tr([pteam[1][q]], slot(0), slot(1), "xf", low))
+        for c, k in relay:
+            send(tr([peerteam[c][1][q]], slot(0), slot(2 + k), "xr%d" % k, low))
+        if direct:
+            send(tr(direct, slot(0), cols(rk), "xland", low))
+        wait(g, ("xf", 8))
+        far = [tr([root], slot(1), cols(fr), "xland", high)]
+        if direct:
+            far.append(tr(direct, slot(1), cols(fr), "xland", low))
+        send(*far)
+        for c, k in relay:
+            wait(g, ("xr%d" % k, 8))
+            send(tr([root], slot(2 + k), cols(T.rank_of(c)), "xland", high),
+                 tr([part], slot(2 + k), cols(T.rank_of(c)), "xland", low))
+        wait(g, ("loc", locn[0]))
+        return
+
+    ci = ctl.index(core)
+    isroot = core == root
+    V, P, S, Y = g.vector, g.tensor, g.scalar, g.sync
+    pool = ["k%d" % i for i in range(90)]
+    ks = lambda: pool.pop(0)
+    erow = lambda t, r: t[128 * r:128 * (r + 1), :]
+    el = low[:4]
+
+    if isroot:
+        Y.dma_start(erow(T.e1all, rk), T.e1[:]).then_inc(sem.e1o, 16)
+        base = ZC + TK * rk
+        for q in range(4):
+            (S if q % 2 == 0 else Y).dma_start(T.land[:, base + XQ * q:base + XQ * (q + 1)],
+                                               T.x[:, XQ * q:XQ * (q + 1)]).then_inc(sem["xl%d" % q], 16)
+        Y.dma_start(erow(T.e2all, rk), T.e2[:]).then_inc(sem.e2o, 16)
+    own = 16 if isroot else 4
+
+    io = ks()
+    fine = dict(allow_small_or_imprecise_dtypes=True)
+    g.iota(T.ip[:], [[0, 144]], 0, 1).then_inc(sem[io], 1)
+    g.iota(T.it[:], [[1, 144]], 0, 0).then_inc(sem[io], 1)
+    g.iota(T.dm[:], [[1, 128]], 0, -1).then_inc(sem[io], 1)
+    g.iota(T.lo[:], [[1, 256]], 0, 0, **fine).then_inc(sem[io], 1)
+    g.iota(T.hif[:], [[1, 4]], ZC // 256 + ci * 16 * SL // 256, 1, **fine).then_inc(sem[io], 1)
+    g.iota(T.trs[:], [[16, SL]], OUT - 8191, 1, **fine).then_inc(sem[io], 1)
+
+    twins = [peerteam[c][0][ci] for c in peers]
+
+    def own_far(e, t):
+        wait(g, (e + "o", own))
+        if isroot:
+            send(tr([c for c in ctl if c != core], erow(t, rk), erow(t, rk), e + "o", high[:4]),
+                 tr(pteam[0], erow(t, rk), erow(t, rk), e + "f", el))
+        send(tr(twins, erow(t, rk), erow(t, rk), e + "p", el))
+
+    def far_on(e, t):
+        wait(g, (e + "f", 4))
+        send(tr(twins, erow(t, fr), erow(t, fr), e + "p", el))
+
+    def xout(q):
+        wait(g, ("xl%d" % q, 16), ("xl%d" % (q + 1), 16))
+        xq = lambda k: T.land[:, ZC + TK * rk + XQ * k:ZC + TK * rk + XQ * (k + 1)]
+        send(tr([car[q]], xq(q), T.xs[0:128, :], "xa", low), tr([car[q + 1]], xq(q + 1), T.xs[0:128, :], "xa", high))
+
+    own_far("e1", T.e1all)
+    if isroot:
+        xout(0)
+    far_on("e1", T.e1all)
+    if isroot:
+        xout(2)
+    own_far("e2", T.e2all)
+    far_on("e2", T.e2all)
+
+    for e, t, w in (("e1", T.e1all, T.e1w), ("e2", T.e2all, T.e2w)):
+        wait(Y, (e + "o", own), (e + "f", 4), (e + "p", 24))
+        Y.dma_start(w[:], t[:]).then_inc(sem[e + "l"], 16)
+
+    def ts(out, in0, s1, op0, s2=None, op1=None):
+        if op1 is None:
+            return V.tensor_scalar(out=out, in0=in0, scalar1=s1, scalar2=None, op0=op0)
+        return V.tensor_scalar(out=out, in0=in0, scalar1=s1, scalar2=s2, op0=op0, op1=op1)
+
+    def tt(out, a, b, o):
+        return V.tensor_tensor(out=out, in0=a, in1=b, op=o)
+
+    fl = ks()
+    nfl = 3 if isroot else 2
+    V.memset(T.ones[:], 1.0).then_inc(sem[fl], 1)
+    V.memset(T.win[:], 0.0).then_inc(sem[fl], 1)
+    if isroot:
+        V.memset(T.land[:, 0:ZC], 0.0).then_inc(sem[fl], 1)
+
+    def level(ins):
+        s = ks()
+        for i in ins:
+            i.then_inc(sem[s], 1)
+        V.wait_ge(sem[s], len(ins))
+        return s, len(ins)
+
+    ib, mb, w0, w1, ww = T.ibm[:, 0:128], T.ibm[:, 128:256], T.wc[:, 0:1], T.wc[:, 1:2], T.wc[:, 2:3]
+    wait(V, (io, 6))
+    level([ts(ib, T.ip[:, 0:128], 4, op.arith_shift_right), ts(mb, T.it[:, 0:128], 4, op.arith_shift_right),
+           ts(T.pm[:], T.ip[:], 15, op.bitwise_and), ts(T.tm[:], T.it[:], 15, op.bitwise_and),
+           ts(T.gtm[:], T.dm[:], 0.0, op.is_lt, -1.0, op.mult), ts(T.d8[:], T.dm[:], 0.0, op.is_equal, BIG, op.mult),
+           ts(T.idm[:], T.dm[:], 0.0, op.is_equal)])
+    level([tt(T.ob[:], ib, mb, op.is_equal), tt(T.lt[:], ib, mb, op.is_lt), ts(T.ar[:], T.pm[:, 0:128], 0.0, op.is_equal),
+           ts(w1, T.pm[:, 0:1], 1.0, op.is_equal), ts(w0, T.pm[:, 0:1], 0.0, op.is_equal, 256.0, op.mult),
+           ts(T.tz[:], T.tm[:], 0.0, op.is_equal)])
+    level([tt(T.rb[:], T.lt[:], T.ar[:], op.mult), tt(T.t2[:], T.gtm[:], T.ob[:], op.mult), tt(ww, w0, w1, op.add),
+           ts(T.hcol[:], T.hif[:], T.ar[:, 0:1], op.mult)])
+    k4 = level([tt(T.kup[:], T.t2[:], T.d8[:], op.add), tt(T.kum[:], T.t2[:], T.d8[:], op.subtract),
+                ts(T.zz[:], T.tz[:], ww, op.mult)]
+               + [ts(T.val[:, 256 * b:256 * (b + 1)], T.lo[:], w1, op.mult, T.hcol[:, b:b + 1], op.add) for b in range(4)])
+    wait(V, (fl, nfl))
+
+    e4 = lambda t, i: t[:, 256 * i:256 * (i + 1)]
+    sx = lambda t, x: t[:, SL * x:SL * (x + 1)]
+    sl = lambda t, x: t[:, 256 * x + SL * ci:256 * x + SL * (ci + 1)]
+    a01, a23, aow = ks(), ks(), ks()
+    wait(V, ("e1l", 16))
+    for i in range(4):
+        ts(e4(T.aa, i), T.e1w[:], float(4 * ci + i), op.is_equal).then_inc(sem[a01 if i < 2 else a23], 1)
+    for x in range(2):
+        ts(e4(T.ao, x), T.e1w[:], float(2 * rk + x), op.is_equal).then_inc(sem[aow], 1)
+    t0, t1, u0, u1, tc, uc = [ks() for _ in range(6)]
+    wait(P, (fl, nfl), k4, (a01, 2))
+    P.matmul(T.pa0[:], T.ob[:], T.aa[:, 0:512], True, True).then_inc(sem[t0], 1)
+    wait(P, (a23, 2))
+    P.matmul(T.pa1[:], T.ob[:], T.aa[:, 512:1024], True, True).then_inc(sem[t1], 1)
+    P.matmul(T.pb0[:], T.kup[:], T.aa[:, 0:512], True, True).then_inc(sem[u0], 1)
+    P.matmul(T.pb1[:], T.kup[:], T.aa[:, 512:1024], True, True).then_inc(sem[u1], 1)
+    wait(P, (aow, 2))
+    P.matmul(T.pc[:], T.ob[:], T.ao[:], True, True).then_inc(sem[tc], 1)
+    for x in range(2):
+        P.matmul(sx(T.pd, x), T.kum[:], sl(T.ao, x), True, True).then_inc(sem[uc], 1)
+
+    def scan(out, d1):
+        return V.tensor_tensor_scan(out, T.ones[:], d1, 0.0, op.mult, op.add)
+
+    s01, s23, be, v0, v1, bc, so_, vo = [ks() for _ in range(8)]
+    for h, ps, tk, sm in ((0, T.pa0, t0, s01), (2, T.pa1, t1, s23)):
+        wait(V, (tk, 1))
+        for i in range(2):
+            scan(e4(T.sf, h + i), e4(ps, i)).then_inc(sem[sm], 1)
+    wait(P, (s01, 2), (s23, 2))
+    P.matmul(T.pe[:, 0:4], T.rb[:], T.sf[:, 255:1024:256], True, True).then_inc(sem[be], 1)
+    wait(V, (s01, 2), (u0, 1))
+    tt(T.vf[:, 0:512], T.sf[:, 0:512], T.pb0[:], op.add).then_inc(sem[v0], 1)
+    wait(V, (be, 1))
+    ts(T.bcol[:], T.pe[:, 0:4], -(BIG + CAP), op.add).then_inc(sem[bc], 1)
+    wait(V, (s23, 2), (u1, 1))
+    tt(T.vf[:, 512:1024], T.sf[:, 512:1024], T.pb1[:], op.add).then_inc(sem[v1], 1)
+    wait(S, (v0, 1), (bc, 1))
+    for i in range(2):
+        S.activation(e4(T.of, i), e4(T.vf, i), AF.Relu, bias=T.bcol[:, i:i + 1]).then_inc(sem[so_], 1)
+    wait(V, (bc, 1), (v1, 1))
+    for i in range(2, 4):
+        ts(e4(T.of, i), e4(T.vf, i), T.bcol[:, i:i + 1], op.add, 0.0, op.max).then_inc(sem[vo], 1)
+    opp, ev = ks(), ks()
+    wait(P, (so_, 2), (vo, 2))
+    for i in range(4):
+        m = P.matmul(T.pf[:, 0:256], T.idm[:], e4(T.of, i), i == 0, i == 3)
+    m.then_inc(sem[opp], 1)
+    wait(S, (opp, 1))
+    S.activation(e4(T.ovl, ci), T.pf[:, 0:256], AF.Copy).then_inc(sem[ev], 1)
+    wait(g, (ev, 1))
+    send(tr([c for c in ctl if c != core], e4(T.ovl, ci), e4(T.ovl, ci), "ovs", high))
+
+    so2, bo, c1k, qk, q1k, ek = [ks() for _ in range(6)]
+    wait(V, (tc, 1))
+    for x in range(2):
+        scan(e4(T.so, x), e4(T.pc, x)).then_inc(sem[so2], 1)
+    wait(P, (so2, 2))
+    P.matmul(T.pa0[:, 0:2], T.rb[:], T.so[:, 255:512:256], True, True).then_inc(sem[bo], 1)
+    P.matmul(T.pa0[:, 2:4], T.ar[:], T.so[:, 255:512:256], True, True).then_inc(sem[bo], 1)
+    wait(V, (so2, 2), (uc, 2))
+    for x in range(2):
+        tt(sx(T.qt, x), sl(T.so, x), sx(T.pd, x), op.add).then_inc(sem[qk], 1)
+    wait(V, (bo, 2), (qk, 2))
+    for x in range(2):
+        ts(T.c1s[:, x:x + 1], T.pa0[:, 2 + x:3 + x], float(CAP), op.min, float(CAP * x), op.add).then_inc(sem[c1k], 1)
+        ts(sx(T.q1, x), sx(T.qt, x), T.pa0[:, x:x + 1], op.add, float(CAP * x), op.add).then_inc(sem[q1k], 1)
+    wait(V, ("e2l", 16))
+    for x in range(2):
+        ts(e4(T.ee, x), T.e2w[:], float(2 * rk + x), op.is_equal).then_inc(sem[ek], 1)
+
+    osk, bk, t2k, u2k, s2k, b2k = [ks() for _ in range(6)]
+    wait(P, (ev, 1), ("ovs", 8 * (NC - 1)))
+    for c in range(NC):
+        m = P.matmul(T.pf[:, 256:512], T.idm[:], e4(T.ovl, c), c == 0, c == NC - 1)
+    m.then_inc(sem[osk], 1)
+    wait(V, (osk, 1), (ek, 2))
+    for x in range(2):
+        tt(e4(T.bb, x), e4(T.ee, x), T.pf[:, 256:512], op.min).then_inc(sem[bk], 1)
+    wait(P, (bk, 2))
+    P.matmul(T.pa1[:], T.ob[:], T.bb[:], True, True).then_inc(sem[t2k], 1)
+    for x in range(2):
+        P.matmul(sx(T.pb0, x), T.kum[:], sl(T.bb, x), True, True).then_inc(sem[u2k], 1)
+    wait(V, (t2k, 1))
+    for x in range(2):
+        scan(e4(T.s2, x), e4(T.pa1, x)).then_inc(sem[s2k], 1)
+    wait(P, (s2k, 2))
+    P.matmul(T.pc[:, 0:2], T.rb[:], T.s2[:, 255:512:256], True, True).then_inc(sem[b2k], 1)
+    f = [ks() for _ in range(9)]
+    wait(V, (s2k, 2), (u2k, 2))
+    for x in range(2):
+        tt(sx(T.uu, x), sl(T.s2, x), sx(T.pb0, x), op.add).then_inc(sem[f[0]], 1)
+    wait(V, (b2k, 1), (f[0], 2), (c1k, 2))
+    for x in range(2):
+        ts(sx(T.uu, 2 + x), sx(T.uu, x), T.pc[:, x:x + 1], op.add, T.c1s[:, x:x + 1], op.add).then_inc(sem[f[1]], 1)
+    wait(V, (f[1], 2), (q1k, 2))
+    tt(T.dd[:], T.uu[:, 2 * SL:4 * SL], T.q1[:], op.min).then_inc(sem[f[2]], 1)
+    wait(V, (f[2], 1))
+    for x in range(2):
+        ts(sx(T.tt, x), sx(T.dd, x), -BIG + CAP * (x + 1), op.is_gt, 2 * BIG, op.mult).then_inc(sem[f[3]], 1)
+    wait(V, (f[3], 2))
+    tt(T.ef[:], T.dd[:], T.tt[:], op.add).then_inc(sem[f[4]], 1)
+    wait(V, (f[4], 1))
+    tt(sx(T.mm, 0), sx(T.ef, 0), sx(T.ef, 1), op.min).then_inc(sem[f[5]], 1)
+    wait(V, (f[5], 1))
+    tt(sx(T.mm, 1), sx(T.mm, 0), T.trs[:], op.min).then_inc(sem[f[6]], 1)
+    wait(V, (f[6], 1))
+    ts(T.offs[:], sx(T.mm, 1), BIG - 1.0, op.add).then_inc(sem[f[7]], 1)
+    wait(V, (f[7], 1))
+    V.tensor_copy(T.win[:].indirect(T.offs[:]), T.val[:]).then_inc(sem[f[8]], 1)
+    lk = ks()
+    wait(P, (f[8], 1))
+    for s in range(16):
+        m = P.matmul(T.pb1[:, 0:LQ], T.zz[:, 16 - s:144 - s], T.win[:, s:OUT:16], s == 0, s == 15)
+    m.then_inc(sem[lk], 1)
+    if not isroot:
+        lc = ks()
+        wait(S, (lk, 1))
+        S.activation(T.ls[:], T.pb1[:, 0:LQ], AF.Copy).then_inc(sem[lc], 1)
+        wait(g, (lc, 1))
+        send(tr([root], T.ls[:], T.lin[:, LQ * (ci - 1):LQ * ci], "li%d" % ci, high))
+        wait(g, ("loc", locn[0]))
+        return
+
+    r1, r2, r3, r4 = [ks() for _ in range(4)]
+    pl = T.pb1[:, 0:LQ]
+    wait(V, (lk, 1), ("li1", 8))
+    tt(pl, pl, T.lin[:, 0:LQ], op.add).then_inc(sem[r1], 1)
+    wait(V, (r1, 1), ("li2", 8))
+    tt(pl, pl, T.lin[:, LQ:2 * LQ], op.add).then_inc(sem[r2], 1)
+    wait(V, (r2, 1), ("li3", 8))
+    tt(T.ls[:], pl, T.lin[:, 2 * LQ:3 * LQ], op.add).then_inc(sem[r3], 1)
+    wait(V, (r3, 1))
+    V.tensor_copy(T.lst[:], T.ls[:]).then_inc(sem[r4], 1)
+    CH, NCH = 40, LQ // 40
+    xw = [("xl%d" % q, 16) for q in range(4)] + [("xland", 8 * NX * (N - 1)), (r4, 1)]
+    gk = [ks() for _ in range(NCH)]
+    wait(V, *xw)
+    wait(S, (fl, nfl), *xw)
+    yc = lambda t, k: t[:, 16 * CH * k:16 * CH * (k + 1)]
+    for k in range(NCH):
+        w = T.land[:].indirect(T.lst[:, CH * k:CH * (k + 1)])
+        if k % 2 == 0:
+            V.tensor_copy(yc(T.ysb, k), w).then_inc(sem[gk[k]], 1)
+        else:
+            S.activation(yc(T.ysb, k), w, AF.Copy).then_inc(sem[gk[k]], 1)
+    for k in range(NCH):
+        q, s = (S, "ysc") if k == NCH - 1 else (Y, "yst")
+        wait(q, (gk[k], 1))
+        q.dma_start(yc(T.y, k), yc(T.ysb, k)).then_inc(sem[s], 16)
+    wait(g, ("yst", 16 * (NCH - 1)), ("ysc", 16), ("loc", locn[0]))

@@ -8,7 +8,8 @@ SL = 256 // NC
 WIN = OUT + 16 * SL + 112
 XQ = TK // NX
 BIG = 8192.0
-VIA_CABLE = ("chip",)
+KINDS = ("host", "chip", "both")
+MATE_OWN, MATE_FAR = ("host", "chip", "both"), ("host", "chip")
 
 _SB = {
     "bfloat16": dict(land=ZC + N * TK, ysb=OUT, lo=256, gtm=128, d8=128, idm=128, ob=128, t2=128, kup=128, kum=128,
@@ -22,11 +23,11 @@ _SB = {
 }
 SCRATCH = {k: ("sbuf", [128, n], d) for d, b in _SB.items() for k, n in b.items()}
 SCRATCH.update({k: ("psum", [128, 512], "float32") for k in ("pa0", "pa1", "pb0", "pb1", "pc", "pd", "pe", "pf")})
-SCRATCH.update({"xs": ("dram", [5 * 128, XQ], "bfloat16"), "e1all": ("dram", [N * 128, 32], "int32"),
+SCRATCH.update({"xs": ("dram", [3 * 128, XQ], "bfloat16"), "e1all": ("dram", [N * 128, 32], "int32"),
                 "e2all": ("dram", [N * 128, 32], "int32")})
-SEMAPHORES = (["e1o", "e1f", "e1p", "e2o", "e2f", "e2p", "e1l", "e2l", "xl0", "xl1", "xl2", "xl3", "xa", "xf", "xr0",
-               "xr1", "xr2", "xland", "loc", "ovs", "li1", "li2", "li3", "yst", "ysc"] + ["k%d" % i for i in range(90)])
-KINDS = ("chip", "host", "both")
+SEMAPHORES = (["e1o", "e1f", "e1p", "e2o", "e2f", "e2p", "e2i", "e1l", "e2l", "xl0", "xl1", "xl2", "xl3", "xa", "xf",
+               "xr0", "xr1", "xr2", "xland", "loc", "ovs", "li1", "li2", "li3", "yst", "ysc"]
+              + ["k%d" % i for i in range(90)])
 
 
 def bits(m):
@@ -41,14 +42,15 @@ def kind(topo, a, b):
 
 def rank_program(g, core, T, topo):
     op, AF = AluOpType, ActivationFunctionType
-    home = [c for c in T.cores if topo.host(c) == topo.host(core) and topo.chip(c) == topo.chip(core)]
+    onchip = lambda a: [c for c in range(512) if topo.host(c) == topo.host(a) and topo.chip(c) == topo.chip(a)]
+    home = [c for c in T.cores if c in onchip(core)] or [c for c in T.cores if topo.mates(core, c)]
     if not home:
         return
     root = home[0]
     rk = T.rank_of(root)
 
     def team(rc):
-        cs = [c for c in range(512) if topo.host(c) == topo.host(rc) and topo.chip(c) == topo.chip(rc)]
+        cs = onchip(rc)
         i = cs.index(rc)
         cs = cs[i:] + cs[:i]
         ctl, car = cs[0::2], cs[1::2]
@@ -56,19 +58,26 @@ def rank_program(g, core, T, topo):
         d1 = [c for c in car if topo.die(c) != topo.die(rc)]
         return ctl, [c for p in zip(d0, d1) for c in p]
 
-    ctl, car = team(root)
+    def relays(rc, die):
+        return [c for c in range(512) if topo.mates(c, rc) and topo.die(c) == die and topo.may_write(c, rc)][:2]
+
     myrack = topo.rack(topo.host(root))
     peers = [c for c in T.cores if c != root and topo.rack(topo.host(c)) == myrack]
+    peers.sort(key=lambda c: KINDS.index(kind(topo, root, c)))
+    kd = [kind(topo, root, c) for c in peers]
     part = [c for c in T.cores if topo.rack(topo.host(c)) != myrack and topo.chip(c) == topo.chip(root)
             and topo.may_write(root, c)][0]
-    fr = T.rank_of(part)
-    pteam = team(part)
-    peerteam = {c: team(c) for c in peers}
 
+    def partner(rc):
+        return [c for c in T.cores if topo.rack(topo.host(c)) != myrack and topo.chip(c) == topo.chip(rc)
+                and topo.may_write(rc, c)][0]
+
+    fr = T.rank_of(part)
+    ctl, car = team(root)
+    pteam = team(part)
+    odd = relays(root, topo.die(root))[0]
+    by_mate = [topo.may_write(c, odd) for c in car]
     sem = T.sem
-    low = bits(topo.mask(core, peers[0]))
-    other = [c for c in ctl if c != core][0]
-    high = [b for b in bits(topo.mask(core, other)) if b not in low]
     locn = [0]
 
     def tr(dcores, src, dst, rsem, engs):
@@ -87,29 +96,51 @@ def rank_program(g, core, T, topo):
         for s, v in pairs:
             q.wait_ge(sem[s], v)
 
-    if core in car:
-        q = car.index(core)
-        cols = lambda s: T.land[:, ZC + TK * s + XQ * q:ZC + TK * s + XQ * (q + 1)]
-        slot = lambda k: T.xs[128 * k:128 * (k + 1), :]
-        direct = [c for c in peers if kind(topo, root, c) not in VIA_CABLE]
-        relay = [(c, KINDS.index(kind(topo, root, c))) for c in peers if kind(topo, root, c) in VIA_CABLE]
-        wait(g, ("xa", 8))
-        send(tr([pteam[1][q]], slot(0), slot(1), "xf", low))
-        for c, k in relay:
-            send(tr([peerteam[c][1][q]], slot(0), slot(2 + k), "xr%d" % k, low))
-        if direct:
-            send(tr(direct, slot(0), cols(rk), "xland", low))
-        wait(g, ("xf", 8))
-        far = [tr([root], slot(1), cols(fr), "xland", high)]
-        if direct:
-            far.append(tr(direct, slot(1), cols(fr), "xland", low))
-        send(*far)
-        for c, k in relay:
-            wait(g, ("xr%d" % k, 8))
-            send(tr([root], slot(2 + k), cols(T.rank_of(c)), "xland", high),
-                 tr([part], slot(2 + k), cols(T.rank_of(c)), "xland", low))
+    slot = lambda k: T.xs[128 * k:128 * (k + 1), :]
+    cols = lambda c, q: T.land[:, ZC + TK * T.rank_of(c) + XQ * q:ZC + TK * T.rank_of(c) + XQ * (q + 1)]
+
+    if topo.mates(core, root):
+        pair = relays(root, topo.die(core))
+        if core not in pair:
+            return
+        far = pair.index(core)
+        q = [i for i in range(NX) if by_mate[i] and topo.die(car[i]) == topo.die(core)][0]
+        for k, c in enumerate(peers):
+            if kd[k] in (MATE_FAR if far else MATE_OWN):
+                wait(g, ("xr%d" % k, 4))
+                send(tr([root], slot(k), cols(partner(c) if far else c, q), "xland", bits(topo.mask(core, root))))
         wait(g, ("loc", locn[0]))
         return
+
+    low = bits(topo.mask(core, peers[0]))
+    other = [c for c in ctl if c != core][0]
+    high = [b for b in bits(topo.mask(core, other)) if b not in low]
+
+    if core in car:
+        q = car.index(core)
+        ea, eb = low[0::2], low[1::2]
+
+        def pass_on(src, c, far, engs):
+            for k, p in enumerate(peers):
+                if by_mate[q] and kd[k] in (MATE_FAR if far else MATE_OWN):
+                    send(tr([relays(p, topo.die(core))[far]], src, slot(k), "xr%d" % k, engs))
+                else:
+                    send(tr([p], src, cols(c, q), "xland", engs))
+
+        wait(g, ("xa", 8))
+        send(tr([pteam[1][q]], slot(0), slot(1), "xf", eb))
+        pass_on(slot(0), root, 0, ea)
+        wait(g, ("xf", 4))
+        pass_on(slot(1), part, 1, eb)
+        send(tr([root], slot(1), cols(part, q), "xland", high))
+        wait(g, ("loc", locn[0]))
+        return
+    nland = 0
+    for q in range(NX):
+        nland += 8
+        for v in kd:
+            nland += 8 if by_mate[q] and v in MATE_OWN else 4
+            nland += 8 if by_mate[q] and v in MATE_FAR else 4
 
     ci = ctl.index(core)
     isroot = core == root
@@ -118,14 +149,14 @@ def rank_program(g, core, T, topo):
     ks = lambda: pool.pop(0)
     erow = lambda t, r: t[128 * r:128 * (r + 1), :]
     el = low[:4]
+    mates4 = [c for c in ctl if c != core]
 
     if isroot:
+        xq = lambda k: cols(root, k)
         Y.dma_start(erow(T.e1all, rk), T.e1[:]).then_inc(sem.e1o, 16)
-        base = ZC + TK * rk
-        for q in range(4):
-            (S if q % 2 == 0 else Y).dma_start(T.land[:, base + XQ * q:base + XQ * (q + 1)],
-                                               T.x[:, XQ * q:XQ * (q + 1)]).then_inc(sem["xl%d" % q], 16)
         Y.dma_start(erow(T.e2all, rk), T.e2[:]).then_inc(sem.e2o, 16)
+        for q in range(4):
+            (S if q % 2 == 0 else Y).dma_start(xq(q), T.x[:, XQ * q:XQ * (q + 1)]).then_inc(sem["xl%d" % q], 16)
     own = 16 if isroot else 4
 
     io = ks()
@@ -137,36 +168,37 @@ def rank_program(g, core, T, topo):
     g.iota(T.hif[:], [[1, 4]], ZC // 256 + ci * 16 * SL // 256, 1, **fine).then_inc(sem[io], 1)
     g.iota(T.trs[:], [[16, SL]], OUT - 8191, 1, **fine).then_inc(sem[io], 1)
 
-    twins = [peerteam[c][0][ci] for c in peers]
-
-    def own_far(e, t):
-        wait(g, (e + "o", own))
-        if isroot:
-            send(tr([c for c in ctl if c != core], erow(t, rk), erow(t, rk), e + "o", high[:4]),
-                 tr(pteam[0], erow(t, rk), erow(t, rk), e + "f", el))
-        send(tr(twins, erow(t, rk), erow(t, rk), e + "p", el))
-
-    def far_on(e, t):
-        wait(g, (e + "f", 4))
-        send(tr(twins, erow(t, fr), erow(t, fr), e + "p", el))
+    twins = [team(c)[0][ci] for c in peers]
+    own1, far1, own2, far2 = erow(T.e1all, rk), erow(T.e1all, fr), erow(T.e2all, rk), erow(T.e2all, fr)
 
     def xout(q):
         wait(g, ("xl%d" % q, 16), ("xl%d" % (q + 1), 16))
-        xq = lambda k: T.land[:, ZC + TK * rk + XQ * k:ZC + TK * rk + XQ * (k + 1)]
-        send(tr([car[q]], xq(q), T.xs[0:128, :], "xa", low), tr([car[q + 1]], xq(q + 1), T.xs[0:128, :], "xa", high))
+        send(tr([car[q]], xq(q), slot(0), "xa", low), tr([car[q + 1]], xq(q + 1), slot(0), "xa", high))
 
-    own_far("e1", T.e1all)
+    wait(g, ("e1o", own))
     if isroot:
+        send(tr(mates4, own1, own1, "e1o", high[:4]), tr(pteam[0], own1, own1, "e1f", el))
+    send(tr(twins, own1, own1, "e1p", el))
+    if isroot:
+        wait(g, ("e2o", 16))
+        send(tr([part], own2, own2, "e2f", el), tr(peers, own2, own2, "e2p", low[4:]))
         xout(0)
-    far_on("e1", T.e1all)
+    wait(g, ("e1f", 4))
+    send(tr(twins, far1, far1, "e1p", el))
     if isroot:
         xout(2)
-    own_far("e2", T.e2all)
-    far_on("e2", T.e2all)
+        wait(g, ("e2f", 4))
+        send(tr(peers, far2, far2, "e2p", low[4:]))
+        wait(g, ("e2p", 24))
+        send(*[tr(mates4, erow(T.e2all, r), erow(T.e2all, r), "e2i", high[r:r + 1]) for r in range(N)])
 
-    for e, t, w in (("e1", T.e1all, T.e1w), ("e2", T.e2all, T.e2w)):
-        wait(Y, (e + "o", own), (e + "f", 4), (e + "p", 24))
-        Y.dma_start(w[:], t[:]).then_inc(sem[e + "l"], 16)
+    wait(Y, ("e1o", own), ("e1f", 4), ("e1p", 24))
+    Y.dma_start(T.e1w[:], T.e1all[:]).then_inc(sem.e1l, 16)
+    if isroot:
+        wait(Y, ("e2o", 16), ("e2f", 4), ("e2p", 24))
+    else:
+        wait(Y, ("e2i", N))
+    Y.dma_start(T.e2w[:], T.e2all[:]).then_inc(sem.e2l, 16)
 
     def ts(out, in0, s1, op0, s2=None, op1=None):
         if op1 is None:
@@ -257,7 +289,7 @@ def rank_program(g, core, T, topo):
     wait(S, (opp, 1))
     S.activation(e4(T.ovl, ci), T.pf[:, 0:256], AF.Copy).then_inc(sem[ev], 1)
     wait(g, (ev, 1))
-    send(tr([c for c in ctl if c != core], e4(T.ovl, ci), e4(T.ovl, ci), "ovs", high))
+    send(tr(mates4, e4(T.ovl, ci), e4(T.ovl, ci), "ovs", high))
 
     so2, bo, c1k, qk, q1k, ek = [ks() for _ in range(6)]
     wait(V, (tc, 1))
@@ -341,7 +373,7 @@ def rank_program(g, core, T, topo):
     wait(V, (r3, 1))
     V.tensor_copy(T.lst[:], T.ls[:]).then_inc(sem[r4], 1)
     CH, NCH = 40, LQ // 40
-    xw = [("xl%d" % q, 16) for q in range(4)] + [("xland", 8 * NX * (N - 1)), (r4, 1)]
+    xw = [("xl%d" % q, 16) for q in range(4)] + [("xland", nland), (r4, 1)]
     gk = [ks() for _ in range(NCH)]
     wait(V, *xw)
     wait(S, (fl, nfl), *xw)

@@ -4,27 +4,31 @@ from concourse.mybir import AluOpType, ActivationFunctionType
 N, TK, CAP, NC, NX, ZC = 8, 4096, 1920, 4, 4, 256
 OUT = 2 * CAP
 LQ = OUT // 16
+NB = OUT // 128
 SL = 256 // NC
 WIN = OUT + 16 * SL + 112
 XQ = TK // NX
 BIG = 8192.0
+E2C = 2
 KINDS = ("host", "chip", "both")
 MATE_OWN, MATE_FAR = ("host", "chip", "both"), ("host", "chip")
 
+_FW = (("pcf", 4), ("rf", 4), ("af", 4), ("w0", 4), ("w1", 4), ("hif", 4), ("hcol", 4), ("hm", 8), ("cc", 2), ("cx", 2),
+       ("sm", 6), ("sm2", 2), ("c1s", 2))
+FO = {k: (sum(w for _, w in _FW[:i]), n) for i, (k, n) in enumerate(_FW)}
 _SB = {
-    "bfloat16": dict(land=ZC + N * TK, ysb=OUT, lo=256, gtm=128, d8=128, idm=128, ob=128, t2=128, kup=128, kum=128,
-                     tz=144, zz=144, ones=256, val=16 * SL, win=WIN, aa=1024, ao=512, of=1024, ovl=NC * 256, ee=512,
-                     bb=512),
-    "int32": dict(e1w=256, e2w=256, ip=144, it=144, dm=128, ibm=256, pm=144, tm=144),
-    "float32": dict(hif=4, trs=SL, lt=128, ar=128, rb=128, wc=3, hcol=4, sf=1024, vf=1024, bcol=4, so=512, c1s=2,
-                    qt=2 * SL, q1=2 * SL, s2=512, uu=4 * SL, dd=2 * SL, tt=2 * SL, ef=2 * SL, mm=2 * SL, ls=LQ,
-                    lin=(NC - 1) * LQ),
+    "bfloat16": dict(land=ZC + N * TK, ysb=OUT, lo=256, gtm=128, nd8=128, idm=128, ob=128, t2=128, kun=128, kum=128,
+                     rm=128, hsel=1024, hl=2, ones=256, val=16 * SL, win=WIN, e1b=256, aa=1024, ao=512, mk=1024,
+                     ovl=NC * 256, ee=512, bb=512, jk=2048, ls=2 * NB, lsum=2 * NB, lin=(NC - 1) * 2 * NB),
+    "int32": dict(ew=512, ip=12, it=128, mb=128, mo=128),
+    "float32": dict(fc=sum(w for _, w in _FW), trs=SL, lt=128, al=128, idf=128, sf=1024, so=512, q1=2 * SL, qt=2 * SL,
+                    qe=2 * SL, s2=512, uu=2 * SL, tt=2 * SL, ef=2 * SL, mm=4 * SL),
     "uint16": dict(offs=SL, lst=LQ),
 }
 SCRATCH = {k: ("sbuf", [128, n], d) for d, b in _SB.items() for k, n in b.items()}
 SCRATCH.update({k: ("psum", [128, 512], "float32") for k in ("pa0", "pa1", "pb0", "pb1", "pc", "pd", "pe", "pf")})
 SCRATCH.update({"xs": ("dram", [3 * 128, XQ], "bfloat16"), "e1all": ("dram", [N * 128, 32], "int32"),
-                "e2all": ("dram", [N * 128, 32], "int32")})
+                "e2all": ("dram", [N * 128, 32], "int32"), "e2s": ("dram", [128, 32], "int32")})
 SEMAPHORES = (["e1o", "e1f", "e1p", "e2o", "e2f", "e2p", "e2i", "e1l", "e2l", "xl0", "xl1", "xl2", "xl3", "xa", "xf",
                "xr0", "xr1", "xr2", "xland", "loc", "ovs", "li1", "li2", "li3", "yst", "ysc"]
               + ["k%d" % i for i in range(90)])
@@ -65,13 +69,12 @@ def rank_program(g, core, T, topo):
     peers = [c for c in T.cores if c != root and topo.rack(topo.host(c)) == myrack]
     peers.sort(key=lambda c: KINDS.index(kind(topo, root, c)))
     kd = [kind(topo, root, c) for c in peers]
-    part = [c for c in T.cores if topo.rack(topo.host(c)) != myrack and topo.chip(c) == topo.chip(root)
-            and topo.may_write(root, c)][0]
 
     def partner(rc):
         return [c for c in T.cores if topo.rack(topo.host(c)) != myrack and topo.chip(c) == topo.chip(rc)
                 and topo.may_write(rc, c)][0]
 
+    part = partner(root)
     fr = T.rank_of(part)
     ctl, car = team(root)
     pteam = team(part)
@@ -115,6 +118,9 @@ def rank_program(g, core, T, topo):
     low = bits(topo.mask(core, peers[0]))
     other = [c for c in ctl if c != core][0]
     high = [b for b in bits(topo.mask(core, other)) if b not in low]
+    erow = lambda t, r: t[128 * r:128 * (r + 1), :]
+    own1, far1, own2, far2 = erow(T.e1all, rk), erow(T.e1all, fr), erow(T.e2all, rk), erow(T.e2all, fr)
+    twins = lambda i: [team(c)[0][i] for c in peers]
 
     if core in car:
         q = car.index(core)
@@ -127,6 +133,8 @@ def rank_program(g, core, T, topo):
                 else:
                     send(tr([p], src, cols(c, q), "xland", engs))
 
+        wait(g, ("e1o", 4))
+        send(tr(twins(q) if q == 0 else twins(q)[2:], own1, own1, "e1p", low))
         wait(g, ("xa", 8))
         send(tr([pteam[1][q]], slot(0), slot(1), "xf", eb))
         pass_on(slot(0), root, 0, ea)
@@ -147,58 +155,67 @@ def rank_program(g, core, T, topo):
     V, P, S, Y = g.vector, g.tensor, g.scalar, g.sync
     pool = ["k%d" % i for i in range(90)]
     ks = lambda: pool.pop(0)
-    erow = lambda t, r: t[128 * r:128 * (r + 1), :]
     el = low[:4]
     mates4 = [c for c in ctl if c != core]
-
-    if isroot:
-        xq = lambda k: cols(root, k)
-        Y.dma_start(erow(T.e1all, rk), T.e1[:]).then_inc(sem.e1o, 16)
-        Y.dma_start(erow(T.e2all, rk), T.e2[:]).then_inc(sem.e2o, 16)
-        for q in range(4):
-            (S if q % 2 == 0 else Y).dma_start(xq(q), T.x[:, XQ * q:XQ * (q + 1)]).then_inc(sem["xl%d" % q], 16)
+    xq = lambda k: cols(root, k)
     own = 16 if isroot else 4
 
-    io = ks()
-    fine = dict(allow_small_or_imprecise_dtypes=True)
-    g.iota(T.ip[:], [[0, 144]], 0, 1).then_inc(sem[io], 1)
-    g.iota(T.it[:], [[1, 144]], 0, 0).then_inc(sem[io], 1)
-    g.iota(T.dm[:], [[1, 128]], 0, -1).then_inc(sem[io], 1)
-    g.iota(T.lo[:], [[1, 256]], 0, 0, **fine).then_inc(sem[io], 1)
-    g.iota(T.hif[:], [[1, 4]], ZC // 256 + ci * 16 * SL // 256, 1, **fine).then_inc(sem[io], 1)
-    g.iota(T.trs[:], [[16, SL]], OUT - 8191, 1, **fine).then_inc(sem[io], 1)
+    def F(name, a=0, n=None):
+        o, w = FO[name]
+        return T.fc[:, o + a:o + a + (w if n is None else n)]
 
-    twins = [team(c)[0][ci] for c in peers]
-    own1, far1, own2, far2 = erow(T.e1all, rk), erow(T.e1all, fr), erow(T.e2all, rk), erow(T.e2all, fr)
+    c1 = lambda name, i=0: F(name, i, 1)
+
+    if isroot:
+        Y.dma_start(own1, T.e1[:]).then_inc(sem.e1o, 16)
+        S.dma_start(T.e2s[:], T.e2[:]).then_inc(sem.e2o, 16)
+        for q in range(4):
+            (S if q % 2 == 0 else Y).dma_start(xq(q), T.x[:, XQ * q:XQ * (q + 1)]).then_inc(sem["xl%d" % q], 16)
+
+    io, io2 = ks(), ks()
+    fine = dict(allow_small_or_imprecise_dtypes=True)
+    g.iota(T.ip[:, 0:4], [[0, 4]], 0, 1).then_inc(sem[io], 1)
+    g.iota(F("pcf"), [[0, 4]], 0, 1, **fine).then_inc(sem[io], 1)
+    g.iota(T.it[:], [[1, 128]], 0, 0).then_inc(sem[io], 1)
+
+    def iotas():
+        g.iota(T.lo[:], [[1, 256]], 0, 0, **fine).then_inc(sem[io2], 1)
+        g.iota(F("hif"), [[1, 4]], ZC // 256 + ci * 16 * SL // 256, 1, **fine).then_inc(sem[io2], 1)
+        g.iota(T.trs[:], [[16, SL]], OUT - 8191, 1, **fine).then_inc(sem[io2], 1)
 
     def xout(q):
         wait(g, ("xl%d" % q, 16), ("xl%d" % (q + 1), 16))
         send(tr([car[q]], xq(q), slot(0), "xa", low), tr([car[q + 1]], xq(q + 1), slot(0), "xa", high))
 
-    wait(g, ("e1o", own))
     if isroot:
-        send(tr(mates4, own1, own1, "e1o", high[:4]), tr(pteam[0], own1, own1, "e1f", el))
-    send(tr(twins, own1, own1, "e1p", el))
-    if isroot:
-        wait(g, ("e2o", 16))
-        send(tr([part], own2, own2, "e2f", el), tr(peers, own2, own2, "e2p", low[4:]))
+        wait(g, ("e1o", 16), ("e2o", 16))
+        send(tr(mates4 + car, own1, own1, "e1o", high[:4]), tr(pteam[0], own1, own1, "e1f", el),
+             tr([ctl[E2C]], T.e2s[:], own2, "e2o", high[4:]), tr([pteam[0][E2C]], T.e2s[:], own2, "e2f", low[4:]))
         xout(0)
-    wait(g, ("e1f", 4))
-    send(tr(twins, far1, far1, "e1p", el))
-    if isroot:
         xout(2)
+        iotas()
+    else:
+        iotas()
+        wait(g, ("e1o", 4))
+        send(tr(twins(ci)[:2], own1, own1, "e1p", el))
+        wait(g, ("e1f", 4))
+        send(tr(twins(ci) + (peers if ci == 1 else []), far1, far1, "e1p", el))
+    if ci == E2C:
+        wait(g, ("e2o", 4))
+        send(tr(twins(ci), own2, own2, "e2p", el))
         wait(g, ("e2f", 4))
-        send(tr(peers, far2, far2, "e2p", low[4:]))
+        send(tr(twins(ci), far2, far2, "e2p", el))
         wait(g, ("e2p", 24))
-        send(*[tr(mates4, erow(T.e2all, r), erow(T.e2all, r), "e2i", high[r:r + 1]) for r in range(N)])
+        send(*[tr(mates4, erow(T.e2all, r), erow(T.e2all, r), "e2i", low[r:r + 1]) for r in range(N)])
 
-    wait(Y, ("e1o", own), ("e1f", 4), ("e1p", 24))
-    Y.dma_start(T.e1w[:], T.e1all[:]).then_inc(sem.e1l, 16)
-    if isroot:
-        wait(Y, ("e2o", 16), ("e2f", 4), ("e2p", 24))
+    e1w, e2w = T.ew[:, 0:256], T.ew[:, 256:512]
+    wait(Y, ("e1o", own), ("e1f", 4), ("e1p", (24 if isroot else 16) + 12))
+    Y.dma_start(e1w, T.e1all[:]).then_inc(sem.e1l, 16)
+    if ci == E2C:
+        wait(Y, ("e2o", 4), ("e2f", 4), ("e2p", 24))
     else:
         wait(Y, ("e2i", N))
-    Y.dma_start(T.e2w[:], T.e2all[:]).then_inc(sem.e2l, 16)
+    Y.dma_start(e2w, T.e2all[:]).then_inc(sem.e2l, 16)
 
     def ts(out, in0, s1, op0, s2=None, op1=None):
         if op1 is None:
@@ -209,11 +226,11 @@ def rank_program(g, core, T, topo):
         return V.tensor_tensor(out=out, in0=a, in1=b, op=o)
 
     fl = ks()
-    nfl = 3 if isroot else 2
-    V.memset(T.ones[:], 1.0).then_inc(sem[fl], 1)
-    V.memset(T.win[:], 0.0).then_inc(sem[fl], 1)
-    if isroot:
-        V.memset(T.land[:, 0:ZC], 0.0).then_inc(sem[fl], 1)
+    fills = [(T.ones[:], 1.0), (T.win[:], 0.0), (T.al[:], 1.0), (F("cc"), -(BIG + CAP)), (c1("cx"), 0.0),
+             (c1("cx", 1), float(CAP))] + ([(T.land[:, 0:ZC], 0.0)] if isroot else [])
+    for t, v in fills:
+        V.memset(t, v).then_inc(sem[fl], 1)
+    nfl = len(fills)
 
     def level(ins):
         s = ks()
@@ -222,156 +239,189 @@ def rank_program(g, core, T, topo):
         V.wait_ge(sem[s], len(ins))
         return s, len(ins)
 
-    ib, mb, w0, w1, ww = T.ibm[:, 0:128], T.ibm[:, 128:256], T.wc[:, 0:1], T.wc[:, 1:2], T.wc[:, 2:3]
-    wait(V, (io, 6))
-    level([ts(ib, T.ip[:, 0:128], 4, op.arith_shift_right), ts(mb, T.it[:, 0:128], 4, op.arith_shift_right),
-           ts(T.pm[:], T.ip[:], 15, op.bitwise_and), ts(T.tm[:], T.it[:], 15, op.bitwise_and),
-           ts(T.gtm[:], T.dm[:], 0.0, op.is_lt, -1.0, op.mult), ts(T.d8[:], T.dm[:], 0.0, op.is_equal, BIG, op.mult),
-           ts(T.idm[:], T.dm[:], 0.0, op.is_equal)])
-    level([tt(T.ob[:], ib, mb, op.is_equal), tt(T.lt[:], ib, mb, op.is_lt), ts(T.ar[:], T.pm[:, 0:128], 0.0, op.is_equal),
-           ts(w1, T.pm[:, 0:1], 1.0, op.is_equal), ts(w0, T.pm[:, 0:1], 0.0, op.is_equal, 256.0, op.mult),
-           ts(T.tz[:], T.tm[:], 0.0, op.is_equal)])
-    level([tt(T.rb[:], T.lt[:], T.ar[:], op.mult), tt(T.t2[:], T.gtm[:], T.ob[:], op.mult), tt(ww, w0, w1, op.add),
-           ts(T.hcol[:], T.hif[:], T.ar[:, 0:1], op.mult)])
-    k4 = level([tt(T.kup[:], T.t2[:], T.d8[:], op.add), tt(T.kum[:], T.t2[:], T.d8[:], op.subtract),
-                ts(T.zz[:], T.tz[:], ww, op.mult)]
-               + [ts(T.val[:, 256 * b:256 * (b + 1)], T.lo[:], w1, op.mult, T.hcol[:, b:b + 1], op.add) for b in range(4)])
+    ip, shi, ai = T.ip[:, 0:4], T.ip[:, 4:8], T.ip[:, 8:12]
+    wait(V, (io, 3))
+    l1 = level([ts(shi, ip, 4, op.arith_shift_right), ts(ai, ip, 15, op.bitwise_and),
+                ts(T.mb[:], T.it[:], 4, op.arith_shift_right), ts(T.mo[:], T.it[:], 15, op.bitwise_and),
+                ts(T.gtm[:], T.it[:], c1("pcf"), op.is_lt, -1.0, op.mult),
+                ts(T.nd8[:], T.it[:], c1("pcf"), op.is_equal, -BIG, op.mult),
+                ts(T.idm[:], T.it[:], c1("pcf"), op.is_equal), ts(T.idf[:], T.it[:], c1("pcf"), op.is_equal)])
+    level([V.tensor_copy(F("rf"), shi), V.tensor_copy(F("af"), ai)])
+    l3 = level([ts(T.ob[:], T.mb[:], c1("rf"), op.is_equal), ts(T.lt[:], T.mb[:], c1("rf"), op.is_gt),
+                ts(F("w0"), F("af"), 0.0, op.is_equal), ts(F("w1"), F("af"), 1.0, op.is_equal),
+                ts(T.hl[:, 0:1], c1("af"), 0.0, op.is_equal, 256.0, op.mult),
+                ts(T.hl[:, 1:2], c1("af"), 1.0, op.is_equal)]
+               + ([ts(T.rm[:], T.mo[:], c1("af"), op.is_equal), ts(F("hm"), T.it[:, 0:8], c1("rf"), op.is_equal)]
+                  if isroot else []))
+    level([tt(T.t2[:], T.gtm[:], T.ob[:], op.mult)])
+    k4 = level([tt(T.kun[:], T.nd8[:], T.t2[:], op.subtract), tt(T.kum[:], T.nd8[:], T.t2[:], op.add)]
+               + ([ts(T.hsel[:, 128 * h:128 * (h + 1)], T.rm[:], c1("hm", h), op.mult) for h in range(8)]
+                  if isroot else []))
+
+    def vals():
+        wait(V, (io2, 3))
+        level([ts(F("hcol"), F("hif"), c1("w0"), op.mult)])
+        level([ts(T.val[:, 256 * b:256 * (b + 1)], T.lo[:], c1("w1"), op.mult, c1("hcol", b), op.add)
+               for b in range(4)])
+
+    if not isroot:
+        vals()
     wait(V, (fl, nfl))
 
     e4 = lambda t, i: t[:, 256 * i:256 * (i + 1)]
     sx = lambda t, x: t[:, SL * x:SL * (x + 1)]
     sl = lambda t, x: t[:, 256 * x + SL * ci:256 * x + SL * (ci + 1)]
-    a01, a23, aow = ks(), ks(), ks()
+    ka, sa = [ks() for _ in range(6)], [ks() for _ in range(6)]
     wait(V, ("e1l", 16))
-    for i in range(4):
-        ts(e4(T.aa, i), T.e1w[:], float(4 * ci + i), op.is_equal).then_inc(sem[a01 if i < 2 else a23], 1)
-    for x in range(2):
-        ts(e4(T.ao, x), T.e1w[:], float(2 * rk + x), op.is_equal).then_inc(sem[aow], 1)
-    t0, t1, u0, u1, tc, uc = [ks() for _ in range(6)]
-    wait(P, (fl, nfl), k4, (a01, 2))
+    level([V.tensor_copy(T.e1b[:], e1w)])
+    ohs = [(e4(T.aa, i), 4 * ci + i) for i in range(4)] + [(e4(T.ao, x), 2 * rk + x) for x in range(2)]
+    for i, (t, k) in enumerate(ohs):
+        ts(t, T.e1b[:], float(k), op.is_equal).then_inc(sem[ka[i]], 1)
+        wait(S, (ka[i], 1))
+        S.activation(e4(T.jk, i), t, AF.Copy, accum_out=c1("sm", i)).then_inc(sem[sa[i]], 1)
+    t0, t1, u0, u1, i01, i23, tc, uc, m01, m23, s01, s23, opp, ev = [ks() for _ in range(14)]
+    wait(P, (fl, nfl), l1, l3, k4)
+    P.matmul(T.pe[:, 0:2], T.idf[:], F("cc"), True, False)
+    P.matmul(T.pd[:, 256:258], T.idf[:], F("cc"), True, False)
+    wait(P, (ka[0], 1), (ka[1], 1))
     P.matmul(T.pa0[:], T.ob[:], T.aa[:, 0:512], True, True).then_inc(sem[t0], 1)
-    wait(P, (a23, 2))
+    wait(P, (sa[0], 1), (sa[1], 1))
+    P.matmul(T.pe[:, 0:2], T.lt[:], F("sm", 0, 2), False, True).then_inc(sem[i01], 1)
+    P.matmul(T.pb0[:], T.kun[:], T.aa[:, 0:512], True, True).then_inc(sem[u0], 1)
+    wait(P, (ka[2], 1), (ka[3], 1))
     P.matmul(T.pa1[:], T.ob[:], T.aa[:, 512:1024], True, True).then_inc(sem[t1], 1)
-    P.matmul(T.pb0[:], T.kup[:], T.aa[:, 0:512], True, True).then_inc(sem[u0], 1)
-    P.matmul(T.pb1[:], T.kup[:], T.aa[:, 512:1024], True, True).then_inc(sem[u1], 1)
-    wait(P, (aow, 2))
-    P.matmul(T.pc[:], T.ob[:], T.ao[:], True, True).then_inc(sem[tc], 1)
-    for x in range(2):
-        P.matmul(sx(T.pd, x), T.kum[:], sl(T.ao, x), True, True).then_inc(sem[uc], 1)
+    wait(P, (sa[2], 1), (sa[3], 1))
+    P.matmul(T.pd[:, 256:258], T.lt[:], F("sm", 2, 2), False, True).then_inc(sem[i23], 1)
+    P.matmul(T.pb1[:], T.kun[:], T.aa[:, 512:1024], True, True).then_inc(sem[u1], 1)
 
-    def scan(out, d1):
-        return V.tensor_tensor_scan(out, T.ones[:], d1, 0.0, op.mult, op.add)
+    def scan(out, d1, init):
+        return V.tensor_tensor_scan(out, T.ones[:], d1, init, op.mult, op.add)
 
-    s01, s23, be, v0, v1, bc, so_, vo = [ks() for _ in range(8)]
-    for h, ps, tk, sm in ((0, T.pa0, t0, s01), (2, T.pa1, t1, s23)):
-        wait(V, (tk, 1))
+    for h, pa, pb, off, tk, ik, uk, sk, mk in ((0, T.pa0, T.pb0, lambda i: T.pe[:, i:i + 1], t0, i01, u0, s01, m01),
+                                               (1, T.pa1, T.pb1, lambda i: T.pd[:, 256 + i:257 + i], t1, i23, u1, s23,
+                                                m23)):
+        wait(V, (tk, 1), (ik, 1))
         for i in range(2):
-            scan(e4(T.sf, h + i), e4(ps, i)).then_inc(sem[sm], 1)
-    wait(P, (s01, 2), (s23, 2))
-    P.matmul(T.pe[:, 0:4], T.rb[:], T.sf[:, 255:1024:256], True, True).then_inc(sem[be], 1)
-    wait(V, (s01, 2), (u0, 1))
-    tt(T.vf[:, 0:512], T.sf[:, 0:512], T.pb0[:], op.add).then_inc(sem[v0], 1)
-    wait(V, (be, 1))
-    ts(T.bcol[:], T.pe[:, 0:4], -(BIG + CAP), op.add).then_inc(sem[bc], 1)
-    wait(V, (s23, 2), (u1, 1))
-    tt(T.vf[:, 512:1024], T.sf[:, 512:1024], T.pb1[:], op.add).then_inc(sem[v1], 1)
-    wait(S, (v0, 1), (bc, 1))
+            scan(e4(T.sf, 2 * h + i), e4(pa, i), off(i)).then_inc(sem[sk], 1)
+        wait(V, (sk, 2), (uk, 1))
+        tt(T.mk[:, 512 * h:512 * (h + 1)], T.sf[:, 512 * h:512 * (h + 1)], pb[:], op.is_gt).then_inc(sem[mk], 1)
+    wait(P, (m01, 1))
     for i in range(2):
-        S.activation(e4(T.of, i), e4(T.vf, i), AF.Relu, bias=T.bcol[:, i:i + 1]).then_inc(sem[so_], 1)
-    wait(V, (bc, 1), (v1, 1))
+        P.matmul(T.pf[:, 0:256], T.idm[:], e4(T.mk, i), i == 0, False)
+    wait(P, (ka[4], 1), (ka[5], 1))
+    P.matmul(T.pc[:], T.ob[:], T.ao[:], True, True).then_inc(sem[tc], 1)
+    wait(P, (m23, 1))
     for i in range(2, 4):
-        ts(e4(T.of, i), e4(T.vf, i), T.bcol[:, i:i + 1], op.add, 0.0, op.max).then_inc(sem[vo], 1)
-    opp, ev = ks(), ks()
-    wait(P, (so_, 2), (vo, 2))
-    for i in range(4):
-        m = P.matmul(T.pf[:, 0:256], T.idm[:], e4(T.of, i), i == 0, i == 3)
+        m = P.matmul(T.pf[:, 0:256], T.idm[:], e4(T.mk, i), False, i == 3)
     m.then_inc(sem[opp], 1)
     wait(S, (opp, 1))
     S.activation(e4(T.ovl, ci), T.pf[:, 0:256], AF.Copy).then_inc(sem[ev], 1)
     wait(g, (ev, 1))
-    send(tr(mates4, e4(T.ovl, ci), e4(T.ovl, ci), "ovs", high))
+    send(tr(mates4, e4(T.ovl, ci), e4(T.ovl, ci), "ovs", low))
 
-    so2, bo, c1k, qk, q1k, ek = [ks() for _ in range(6)]
-    wait(V, (tc, 1))
+    wait(P, (s01, 2), (s23, 2), (sa[4], 1), (sa[5], 1))
     for x in range(2):
-        scan(e4(T.so, x), e4(T.pc, x)).then_inc(sem[so2], 1)
-    wait(P, (so2, 2))
-    P.matmul(T.pa0[:, 0:2], T.rb[:], T.so[:, 255:512:256], True, True).then_inc(sem[bo], 1)
-    P.matmul(T.pa0[:, 2:4], T.ar[:], T.so[:, 255:512:256], True, True).then_inc(sem[bo], 1)
-    wait(V, (so2, 2), (uc, 2))
+        P.matmul(sx(T.pd, x), T.kum[:], sl(T.ao, x), True, True).then_inc(sem[uc], 1)
+    P.matmul(T.pd[:, 128:130], T.idf[:], F("cx"), True, False)
+    P.matmul(T.pd[:, 128:130], T.lt[:], F("sm", 4, 2), False, True).then_inc(sem[uc], 1)
+    P.matmul(T.pd[:, 130:132], T.al[:], F("sm", 4, 2), True, True).then_inc(sem[uc], 1)
+    so2, c1k, qk, ek, f1, f2, f3, f4 = [ks() for _ in range(8)]
+    lim = lambda x: -BIG + CAP * (x + 1)
+    if isroot:
+        vals()
+    wait(V, (tc, 1), (uc, 4))
     for x in range(2):
-        tt(sx(T.qt, x), sl(T.so, x), sx(T.pd, x), op.add).then_inc(sem[qk], 1)
-    wait(V, (bo, 2), (qk, 2))
+        scan(e4(T.so, x), e4(T.pc, x), T.pd[:, 128 + x:129 + x]).then_inc(sem[so2], 1)
     for x in range(2):
-        ts(T.c1s[:, x:x + 1], T.pa0[:, 2 + x:3 + x], float(CAP), op.min, float(CAP * x), op.add).then_inc(sem[c1k], 1)
-        ts(sx(T.q1, x), sx(T.qt, x), T.pa0[:, x:x + 1], op.add, float(CAP * x), op.add).then_inc(sem[q1k], 1)
+        ts(c1("c1s", x), T.pd[:, 130 + x:131 + x], float(CAP), op.min, float(CAP * x), op.add).then_inc(sem[c1k], 1)
+    wait(V, (so2, 2))
+    for x in range(2):
+        tt(sx(T.q1, x), sl(T.so, x), sx(T.pd, x), op.add).then_inc(sem[qk], 1)
+    wait(V, (qk, 2))
+    for x in range(2):
+        ts(sx(T.qt, x), sx(T.q1, x), lim(x), op.is_gt, 2 * BIG, op.mult).then_inc(sem[f1], 1)
+    wait(V, (f1, 2))
+    tt(T.qe[:], T.q1[:], T.qt[:], op.add).then_inc(sem[f2], 1)
+    wait(V, (f2, 1))
+    tt(sx(T.mm, 2), sx(T.qe, 0), sx(T.qe, 1), op.min).then_inc(sem[f3], 1)
+    wait(V, (f3, 1))
+    tt(sx(T.mm, 3), sx(T.mm, 2), T.trs[:], op.min).then_inc(sem[f4], 1)
     wait(V, ("e2l", 16))
     for x in range(2):
-        ts(e4(T.ee, x), T.e2w[:], float(2 * rk + x), op.is_equal).then_inc(sem[ek], 1)
+        ts(e4(T.ee, x), e2w, float(2 * rk + x), op.is_equal).then_inc(sem[ek], 1)
 
-    osk, bk, t2k, u2k, s2k, b2k = [ks() for _ in range(6)]
-    wait(P, (ev, 1), ("ovs", 8 * (NC - 1)))
-    for c in range(NC):
-        m = P.matmul(T.pf[:, 256:512], T.idm[:], e4(T.ovl, c), c == 0, c == NC - 1)
+    osk, u2k, s2k = [ks() for _ in range(3)]
+    bk, sk2, tk2, ik2 = [[ks(), ks()] for _ in range(4)]
+    f = [ks() for _ in range(7)]
+    wait(P, (ev, 1))
+    P.matmul(T.pf[:, 256:512], T.idm[:], e4(T.ovl, ci), True, False)
+    wait(P, (so2, 2), (c1k, 2), (qk, 2))
+    ini = (T.pc[:, 0:1], T.pd[:, 0:1])
+    for x in range(2):
+        P.matmul(ini[x], T.idf[:], c1("c1s", x), True, False)
+    wait(P, ("ovs", 8 * (NC - 1)))
+    oth = [c for c in range(NC) if c != ci]
+    for c in oth:
+        m = P.matmul(T.pf[:, 256:512], T.idm[:], e4(T.ovl, c), False, c == oth[-1])
     m.then_inc(sem[osk], 1)
     wait(V, (osk, 1), (ek, 2))
     for x in range(2):
-        tt(e4(T.bb, x), e4(T.ee, x), T.pf[:, 256:512], op.min).then_inc(sem[bk], 1)
-    wait(P, (bk, 2))
-    P.matmul(T.pa1[:], T.ob[:], T.bb[:], True, True).then_inc(sem[t2k], 1)
-    for x in range(2):
+        tt(e4(T.bb, x), e4(T.ee, x), T.pf[:, 256:512], op.min).then_inc(sem[bk[x]], 1)
+    for x, pa in ((0, T.pa0), (1, T.pa1)):
+        wait(S, (bk[x], 1))
+        S.activation(e4(T.jk, 6 + x), e4(T.bb, x), AF.Copy, accum_out=c1("sm2", x)).then_inc(sem[sk2[x]], 1)
+        wait(P, (bk[x], 1))
+        P.matmul(pa[:, 0:256], T.ob[:], e4(T.bb, x), True, True).then_inc(sem[tk2[x]], 1)
         P.matmul(sx(T.pb0, x), T.kum[:], sl(T.bb, x), True, True).then_inc(sem[u2k], 1)
-    wait(V, (t2k, 1))
-    for x in range(2):
-        scan(e4(T.s2, x), e4(T.pa1, x)).then_inc(sem[s2k], 1)
-    wait(P, (s2k, 2))
-    P.matmul(T.pc[:, 0:2], T.rb[:], T.s2[:, 255:512:256], True, True).then_inc(sem[b2k], 1)
-    f = [ks() for _ in range(9)]
+        wait(P, (sk2[x], 1))
+        P.matmul(ini[x], T.lt[:], c1("sm2", x), False, True).then_inc(sem[ik2[x]], 1)
+        wait(V, (tk2[x], 1), (ik2[x], 1))
+        scan(e4(T.s2, x), pa[:, 0:256], ini[x]).then_inc(sem[s2k], 1)
     wait(V, (s2k, 2), (u2k, 2))
     for x in range(2):
         tt(sx(T.uu, x), sl(T.s2, x), sx(T.pb0, x), op.add).then_inc(sem[f[0]], 1)
-    wait(V, (b2k, 1), (f[0], 2), (c1k, 2))
+    wait(V, (f[0], 2))
     for x in range(2):
-        ts(sx(T.uu, 2 + x), sx(T.uu, x), T.pc[:, x:x + 1], op.add, T.c1s[:, x:x + 1], op.add).then_inc(sem[f[1]], 1)
-    wait(V, (f[1], 2), (q1k, 2))
-    tt(T.dd[:], T.uu[:, 2 * SL:4 * SL], T.q1[:], op.min).then_inc(sem[f[2]], 1)
+        ts(sx(T.tt, x), sx(T.uu, x), lim(x), op.is_gt, 2 * BIG, op.mult).then_inc(sem[f[1]], 1)
+    wait(V, (f[1], 2))
+    tt(T.ef[:], T.uu[:], T.tt[:], op.add).then_inc(sem[f[2]], 1)
     wait(V, (f[2], 1))
-    for x in range(2):
-        ts(sx(T.tt, x), sx(T.dd, x), -BIG + CAP * (x + 1), op.is_gt, 2 * BIG, op.mult).then_inc(sem[f[3]], 1)
-    wait(V, (f[3], 2))
-    tt(T.ef[:], T.dd[:], T.tt[:], op.add).then_inc(sem[f[4]], 1)
+    tt(sx(T.mm, 0), sx(T.ef, 0), sx(T.ef, 1), op.min).then_inc(sem[f[3]], 1)
+    wait(V, (f[3], 1), (f4, 1))
+    tt(sx(T.mm, 1), sx(T.mm, 0), sx(T.mm, 3), op.min).then_inc(sem[f[4]], 1)
     wait(V, (f[4], 1))
-    tt(sx(T.mm, 0), sx(T.ef, 0), sx(T.ef, 1), op.min).then_inc(sem[f[5]], 1)
+    ts(T.offs[:], sx(T.mm, 1), BIG - 1.0, op.add).then_inc(sem[f[5]], 1)
     wait(V, (f[5], 1))
-    tt(sx(T.mm, 1), sx(T.mm, 0), T.trs[:], op.min).then_inc(sem[f[6]], 1)
-    wait(V, (f[6], 1))
-    ts(T.offs[:], sx(T.mm, 1), BIG - 1.0, op.add).then_inc(sem[f[7]], 1)
-    wait(V, (f[7], 1))
-    V.tensor_copy(T.win[:].indirect(T.offs[:]), T.val[:]).then_inc(sem[f[8]], 1)
-    lk = ks()
-    wait(P, (f[8], 1))
-    for s in range(16):
-        m = P.matmul(T.pb1[:, 0:LQ], T.zz[:, 16 - s:144 - s], T.win[:, s:OUT:16], s == 0, s == 15)
+    V.tensor_copy(T.win[:].indirect(T.offs[:]), T.val[:]).then_inc(sem[f[6]], 1)
+    lk, lc = ks(), ks()
+    wait(P, (f[6], 1))
+    for b in range(NB):
+        m = P.matmul(T.pb1[:, 2 * b:2 * b + 2], T.win[:, 128 * b:128 * (b + 1)], T.hl[:], True, True)
     m.then_inc(sem[lk], 1)
+    wait(S, (lk, 1))
+    S.activation(T.ls[:], T.pb1[:, 0:2 * NB], AF.Copy).then_inc(sem[lc], 1)
     if not isroot:
-        lc = ks()
-        wait(S, (lk, 1))
-        S.activation(T.ls[:], T.pb1[:, 0:LQ], AF.Copy).then_inc(sem[lc], 1)
         wait(g, (lc, 1))
-        send(tr([root], T.ls[:], T.lin[:, LQ * (ci - 1):LQ * ci], "li%d" % ci, high))
+        send(tr([root], T.ls[:], T.lin[:, 2 * NB * (ci - 1):2 * NB * ci], "li%d" % ci, low))
         wait(g, ("loc", locn[0]))
         return
 
     r1, r2, r3, r4 = [ks() for _ in range(4)]
-    pl = T.pb1[:, 0:LQ]
-    wait(V, (lk, 1), ("li1", 8))
-    tt(pl, pl, T.lin[:, 0:LQ], op.add).then_inc(sem[r1], 1)
-    wait(V, (r1, 1), ("li2", 8))
-    tt(pl, pl, T.lin[:, LQ:2 * LQ], op.add).then_inc(sem[r2], 1)
-    wait(V, (r2, 1), ("li3", 8))
-    tt(T.ls[:], pl, T.lin[:, 2 * LQ:3 * LQ], op.add).then_inc(sem[r3], 1)
+    wait(P, (lc, 1))
+    P.matmul(T.pe[:, 0:2 * NB], T.idm[:], T.ls[:], True, False)
+    for c in range(1, NC):
+        wait(P, ("li%d" % c, 8))
+        m = P.matmul(T.pe[:, 0:2 * NB], T.idm[:], T.lin[:, 2 * NB * (c - 1):2 * NB * c], False, c == NC - 1)
+    m.then_inc(sem[r1], 1)
+    wait(V, (r1, 1))
+    V.tensor_copy(T.lsum[:], T.pe[:, 0:2 * NB]).then_inc(sem[r2], 1)
+    wait(P, (r2, 1))
+    for h in range(8):
+        for i in range(2):
+            m = P.matmul(T.pf[:, h:LQ:8], T.hsel[:, 128 * h:128 * (h + 1)], T.lsum[:, i:2 * NB:2], i == 0, i == 1)
+    m.then_inc(sem[r3], 1)
     wait(V, (r3, 1))
-    V.tensor_copy(T.lst[:], T.ls[:]).then_inc(sem[r4], 1)
+    V.tensor_copy(T.lst[:], T.pf[:, 0:LQ]).then_inc(sem[r4], 1)
     CH, NCH = 40, LQ // 40
     xw = [("xl%d" % q, 16) for q in range(4)] + [("xland", nland), (r4, 1)]
     gk = [ks() for _ in range(NCH)]

from concourse.bass import DstId, RemoteDMATransfer
from concourse.mybir import AluOpType, ActivationFunctionType

N, TK, CAP, NC, NX, ZC = 8, 4096, 1920, 4, 4, 256
OUT = 2 * CAP
LQ = OUT // 16
NB = OUT // 128
SL = 256 // NC
WIN = OUT + 16 * SL + 112
XQ = TK // NX
BIG = 8192.0
E2C = 2
KINDS = ("host", "chip", "both")
MATE_OWN, MATE_FAR = ("host", "chip", "both"), ("host", "chip")

_FW = (("pcf", 4), ("rf", 4), ("af", 4), ("w0", 4), ("w1", 4), ("hif", 4), ("hcol", 4), ("hm", 8), ("cc", 2), ("cx", 2),
       ("sm", 6), ("sm2", 2), ("c1s", 2))
FO = {k: (sum(w for _, w in _FW[:i]), n) for i, (k, n) in enumerate(_FW)}
_SB = {
    "bfloat16": dict(land=ZC + N * TK, ysb=OUT, lo=256, gtm=128, nd8=128, idm=128, ob=128, t2=128, kun=128, kum=128,
                     rm=128, hsel=1024, hl=2, ones=256, val=16 * SL, win=WIN, e1b=256, aa=1024, ao=512, mk=1024,
                     ovl=NC * 256, ee=512, bb=512, jk=2048, ls=2 * NB, lsum=2 * NB, lin=(NC - 1) * 2 * NB),
    "int32": dict(ew=512, ip=12, it=128, mb=128, mo=128),
    "float32": dict(fc=sum(w for _, w in _FW), trs=SL, lt=128, al=128, idf=128, sf=1024, so=512, q1=2 * SL, qt=2 * SL,
                    qe=2 * SL, s2=512, uu=2 * SL, tt=2 * SL, ef=2 * SL, mm=4 * SL),
    "uint16": dict(offs=SL, lst=LQ),
}
SCRATCH = {k: ("sbuf", [128, n], d) for d, b in _SB.items() for k, n in b.items()}
SCRATCH.update({k: ("psum", [128, 512], "float32") for k in ("pa0", "pa1", "pb0", "pb1", "pc", "pd", "pe", "pf")})
SCRATCH.update({"xs": ("dram", [3 * 128, XQ], "bfloat16"), "e1all": ("dram", [N * 128, 32], "int32"),
                "e2all": ("dram", [N * 128, 32], "int32"), "e2s": ("dram", [128, 32], "int32")})
SEMAPHORES = (["e1o", "e1f", "e1p", "e2o", "e2f", "e2p", "e2i", "e1l", "e2l", "xl0", "xl1", "xl2", "xl3", "xa", "xf",
               "xr0", "xr1", "xr2", "xland", "loc", "ovs", "li1", "li2", "li3", "yst", "ysc"]
              + ["k%d" % i for i in range(90)])


def bits(m):
    return [1 << i for i in range(16) if m >> i & 1]


def kind(topo, a, b):
    if topo.host(a) == topo.host(b):
        return "chip"
    return "host" if topo.chip(a) == topo.chip(b) else "both"


def rank_program(g, core, T, topo):
    op, AF = AluOpType, ActivationFunctionType
    onchip = lambda a: [c for c in range(512) if topo.host(c) == topo.host(a) and topo.chip(c) == topo.chip(a)]
    home = [c for c in T.cores if c in onchip(core)] or [c for c in T.cores if topo.mates(core, c)]
    if not home:
        return
    root = home[0]
    rk = T.rank_of(root)

    def team(rc):
        cs = onchip(rc)
        i = cs.index(rc)
        cs = cs[i:] + cs[:i]
        ctl, car = cs[0::2], cs[1::2]
        d0 = [c for c in car if topo.die(c) == topo.die(rc)]
        d1 = [c for c in car if topo.die(c) != topo.die(rc)]
        return ctl, [c for p in zip(d0, d1) for c in p]

    def relays(rc, die):
        return [c for c in range(512) if topo.mates(c, rc) and topo.die(c) == die and topo.may_write(c, rc)][:2]

    myrack = topo.rack(topo.host(root))
    peers = [c for c in T.cores if c != root and topo.rack(topo.host(c)) == myrack]
    peers.sort(key=lambda c: KINDS.index(kind(topo, root, c)))
    kd = [kind(topo, root, c) for c in peers]

    def partner(rc):
        return [c for c in T.cores if topo.rack(topo.host(c)) != myrack and topo.chip(c) == topo.chip(rc)
                and topo.may_write(rc, c)][0]

    part = partner(root)
    fr = T.rank_of(part)
    ctl, car = team(root)
    pteam = team(part)
    odd = relays(root, topo.die(root))[0]
    by_mate = [topo.may_write(c, odd) for c in car]
    sem = T.sem
    locn = [0]

    def tr(dcores, src, dst, rsem, engs):
        ids = []
        for c in dcores:
            rid, pid = topo.addr(c, core)
            ids.append(DstId(rid=rid, pnc=pid))
        locn[0] += len(engs)
        return RemoteDMATransfer(dst_ids=ids, dma_engine_mask=sum(engs), remote_sem=sem[rsem], srcs=[src],
                                 dsts=[dst] * len(ids))

    def send(*trs):
        g.remote_dma_fused(list(trs), local_sem=sem.loc)

    def wait(q, *pairs):
        for s, v in pairs:
            q.wait_ge(sem[s], v)

    slot = lambda k: T.xs[128 * k:128 * (k + 1), :]
    cols = lambda c, q: T.land[:, ZC + TK * T.rank_of(c) + XQ * q:ZC + TK * T.rank_of(c) + XQ * (q + 1)]

    if topo.mates(core, root):
        pair = relays(root, topo.die(core))
        if core not in pair:
            return
        far = pair.index(core)
        q = [i for i in range(NX) if by_mate[i] and topo.die(car[i]) == topo.die(core)][0]
        for k, c in enumerate(peers):
            if kd[k] in (MATE_FAR if far else MATE_OWN):
                wait(g, ("xr%d" % k, 4))
                send(tr([root], slot(k), cols(partner(c) if far else c, q), "xland", bits(topo.mask(core, root))))
        wait(g, ("loc", locn[0]))
        return

    low = bits(topo.mask(core, peers[0]))
    other = [c for c in ctl if c != core][0]
    high = [b for b in bits(topo.mask(core, other)) if b not in low]
    erow = lambda t, r: t[128 * r:128 * (r + 1), :]
    own1, far1, own2, far2 = erow(T.e1all, rk), erow(T.e1all, fr), erow(T.e2all, rk), erow(T.e2all, fr)
    twins = lambda i: [team(c)[0][i] for c in peers]

    if core in car:
        q = car.index(core)
        ea, eb = low[0::2], low[1::2]

        def pass_on(src, c, far, engs):
            for k, p in enumerate(peers):
                if by_mate[q] and kd[k] in (MATE_FAR if far else MATE_OWN):
                    send(tr([relays(p, topo.die(core))[far]], src, slot(k), "xr%d" % k, engs))
                else:
                    send(tr([p], src, cols(c, q), "xland", engs))

        wait(g, ("e1o", 4))
        send(tr(twins(q) if q == 0 else twins(q)[2:], own1, own1, "e1p", low))
        wait(g, ("xa", 8))
        send(tr([pteam[1][q]], slot(0), slot(1), "xf", eb))
        pass_on(slot(0), root, 0, ea)
        wait(g, ("xf", 4))
        pass_on(slot(1), part, 1, eb)
        send(tr([root], slot(1), cols(part, q), "xland", high))
        wait(g, ("loc", locn[0]))
        return
    nland = 0
    for q in range(NX):
        nland += 8
        for v in kd:
            nland += 8 if by_mate[q] and v in MATE_OWN else 4
            nland += 8 if by_mate[q] and v in MATE_FAR else 4

    ci = ctl.index(core)
    isroot = core == root
    V, P, S, Y = g.vector, g.tensor, g.scalar, g.sync
    pool = ["k%d" % i for i in range(90)]
    ks = lambda: pool.pop(0)
    el = low[:4]
    mates4 = [c for c in ctl if c != core]
    xq = lambda k: cols(root, k)
    own = 16 if isroot else 4

    def F(name, a=0, n=None):
        o, w = FO[name]
        return T.fc[:, o + a:o + a + (w if n is None else n)]

    c1 = lambda name, i=0: F(name, i, 1)

    if isroot:
        Y.dma_start(own1, T.e1[:]).then_inc(sem.e1o, 16)
        S.dma_start(T.e2s[:], T.e2[:]).then_inc(sem.e2o, 16)
        for q in range(4):
            (S if q % 2 == 0 else Y).dma_start(xq(q), T.x[:, XQ * q:XQ * (q + 1)]).then_inc(sem["xl%d" % q], 16)

    io, io2 = ks(), ks()
    fine = dict(allow_small_or_imprecise_dtypes=True)
    g.iota(T.ip[:, 0:4], [[0, 4]], 0, 1).then_inc(sem[io], 1)
    g.iota(F("pcf"), [[0, 4]], 0, 1, **fine).then_inc(sem[io], 1)
    g.iota(T.it[:], [[1, 128]], 0, 0).then_inc(sem[io], 1)

    def iotas():
        g.iota(T.lo[:], [[1, 256]], 0, 0, **fine).then_inc(sem[io2], 1)
        g.iota(F("hif"), [[1, 4]], ZC // 256 + ci * 16 * SL // 256, 1, **fine).then_inc(sem[io2], 1)
        g.iota(T.trs[:], [[16, SL]], OUT - 8191, 1, **fine).then_inc(sem[io2], 1)

    def xout(q):
        wait(g, ("xl%d" % q, 16), ("xl%d" % (q + 1), 16))
        send(tr([car[q]], xq(q), slot(0), "xa", low), tr([car[q + 1]], xq(q + 1), slot(0), "xa", high))

    if isroot:
        wait(g, ("e1o", 16), ("e2o", 16))
        send(tr(mates4 + car, own1, own1, "e1o", high[:4]), tr(pteam[0], own1, own1, "e1f", el),
             tr([ctl[E2C]], T.e2s[:], own2, "e2o", high[4:]), tr([pteam[0][E2C]], T.e2s[:], own2, "e2f", low[4:]))
        xout(0)
        xout(2)
        iotas()
    else:
        iotas()
        wait(g, ("e1o", 4))
        send(tr(twins(ci)[:2], own1, own1, "e1p", el))
        wait(g, ("e1f", 4))
        send(tr(twins(ci) + (peers if ci == 1 else []), far1, far1, "e1p", el))
    if ci == E2C:
        wait(g, ("e2o", 4))
        send(tr(twins(ci), own2, own2, "e2p", el))
        wait(g, ("e2f", 4))
        send(tr(twins(ci), far2, far2, "e2p", el))
        wait(g, ("e2p", 24))
        send(*[tr(mates4, erow(T.e2all, r), erow(T.e2all, r), "e2i", low[r:r + 1]) for r in range(N)])

    e1w, e2w = T.ew[:, 0:256], T.ew[:, 256:512]
    wait(Y, ("e1o", own), ("e1f", 4), ("e1p", (24 if isroot else 16) + 12))
    Y.dma_start(e1w, T.e1all[:]).then_inc(sem.e1l, 16)
    if ci == E2C:
        wait(Y, ("e2o", 4), ("e2f", 4), ("e2p", 24))
    else:
        wait(Y, ("e2i", N))
    Y.dma_start(e2w, T.e2all[:]).then_inc(sem.e2l, 16)

    def ts(out, in0, s1, op0, s2=None, op1=None):
        if op1 is None:
            return V.tensor_scalar(out=out, in0=in0, scalar1=s1, scalar2=None, op0=op0)
        return V.tensor_scalar(out=out, in0=in0, scalar1=s1, scalar2=s2, op0=op0, op1=op1)

    def tt(out, a, b, o):
        return V.tensor_tensor(out=out, in0=a, in1=b, op=o)

    fl = ks()
    fills = [(T.ones[:], 1.0), (T.win[:], 0.0), (T.al[:], 1.0), (F("cc"), -(BIG + CAP)), (c1("cx"), 0.0),
             (c1("cx", 1), float(CAP))] + ([(T.land[:, 0:ZC], 0.0)] if isroot else [])
    for t, v in fills:
        V.memset(t, v).then_inc(sem[fl], 1)
    nfl = len(fills)

    def level(ins):
        s = ks()
        for i in ins:
            i.then_inc(sem[s], 1)
        V.wait_ge(sem[s], len(ins))
        return s, len(ins)

    ip, shi, ai = T.ip[:, 0:4], T.ip[:, 4:8], T.ip[:, 8:12]
    wait(V, (io, 3))
    l1 = level([ts(shi, ip, 4, op.arith_shift_right), ts(ai, ip, 15, op.bitwise_and),
                ts(T.mb[:], T.it[:], 4, op.arith_shift_right), ts(T.mo[:], T.it[:], 15, op.bitwise_and),
                ts(T.gtm[:], T.it[:], c1("pcf"), op.is_lt, -1.0, op.mult),
                ts(T.nd8[:], T.it[:], c1("pcf"), op.is_equal, -BIG, op.mult),
                ts(T.idm[:], T.it[:], c1("pcf"), op.is_equal), ts(T.idf[:], T.it[:], c1("pcf"), op.is_equal)])
    level([V.tensor_copy(F("rf"), shi), V.tensor_copy(F("af"), ai)])
    l3 = level([ts(T.ob[:], T.mb[:], c1("rf"), op.is_equal), ts(T.lt[:], T.mb[:], c1("rf"), op.is_gt),
                ts(F("w0"), F("af"), 0.0, op.is_equal), ts(F("w1"), F("af"), 1.0, op.is_equal),
                ts(T.hl[:, 0:1], c1("af"), 0.0, op.is_equal, 256.0, op.mult),
                ts(T.hl[:, 1:2], c1("af"), 1.0, op.is_equal)]
               + ([ts(T.rm[:], T.mo[:], c1("af"), op.is_equal), ts(F("hm"), T.it[:, 0:8], c1("rf"), op.is_equal)]
                  if isroot else []))
    level([tt(T.t2[:], T.gtm[:], T.ob[:], op.mult)])
    k4 = level([tt(T.kun[:], T.nd8[:], T.t2[:], op.subtract), tt(T.kum[:], T.nd8[:], T.t2[:], op.add)]
               + ([ts(T.hsel[:, 128 * h:128 * (h + 1)], T.rm[:], c1("hm", h), op.mult) for h in range(8)]
                  if isroot else []))

    def vals():
        wait(V, (io2, 3))
        level([ts(F("hcol"), F("hif"), c1("w0"), op.mult)])
        level([ts(T.val[:, 256 * b:256 * (b + 1)], T.lo[:], c1("w1"), op.mult, c1("hcol", b), op.add)
               for b in range(4)])

    if not isroot:
        vals()
    wait(V, (fl, nfl))

    e4 = lambda t, i: t[:, 256 * i:256 * (i + 1)]
    sx = lambda t, x: t[:, SL * x:SL * (x + 1)]
    sl = lambda t, x: t[:, 256 * x + SL * ci:256 * x + SL * (ci + 1)]
    ka, sa = [ks() for _ in range(6)], [ks() for _ in range(6)]
    wait(V, ("e1l", 16))
    level([V.tensor_copy(T.e1b[:], e1w)])
    ohs = [(e4(T.aa, i), 4 * ci + i) for i in range(4)] + [(e4(T.ao, x), 2 * rk + x) for x in range(2)]
    for i, (t, k) in enumerate(ohs):
        ts(t, T.e1b[:], float(k), op.is_equal).then_inc(sem[ka[i]], 1)
        wait(S, (ka[i], 1))
        S.activation(e4(T.jk, i), t, AF.Copy, accum_out=c1("sm", i)).then_inc(sem[sa[i]], 1)
    t0, t1, u0, u1, i01, i23, tc, uc, m01, m23, s01, s23, opp, ev = [ks() for _ in range(14)]
    wait(P, (fl, nfl), l1, l3, k4)
    P.matmul(T.pe[:, 0:2], T.idf[:], F("cc"), True, False)
    P.matmul(T.pd[:, 256:258], T.idf[:], F("cc"), True, False)
    wait(P, (ka[0], 1), (ka[1], 1))
    P.matmul(T.pa0[:], T.ob[:], T.aa[:, 0:512], True, True).then_inc(sem[t0], 1)
    wait(P, (sa[0], 1), (sa[1], 1))
    P.matmul(T.pe[:, 0:2], T.lt[:], F("sm", 0, 2), False, True).then_inc(sem[i01], 1)
    P.matmul(T.pb0[:], T.kun[:], T.aa[:, 0:512], True, True).then_inc(sem[u0], 1)
    wait(P, (ka[2], 1), (ka[3], 1))
    P.matmul(T.pa1[:], T.ob[:], T.aa[:, 512:1024], True, True).then_inc(sem[t1], 1)
    wait(P, (sa[2], 1), (sa[3], 1))
    P.matmul(T.pd[:, 256:258], T.lt[:], F("sm", 2, 2), False, True).then_inc(sem[i23], 1)
    P.matmul(T.pb1[:], T.kun[:], T.aa[:, 512:1024], True, True).then_inc(sem[u1], 1)

    def scan(out, d1, init):
        return V.tensor_tensor_scan(out, T.ones[:], d1, init, op.mult, op.add)

    for h, pa, pb, off, tk, ik, uk, sk, mk in ((0, T.pa0, T.pb0, lambda i: T.pe[:, i:i + 1], t0, i01, u0, s01, m01),
                                               (1, T.pa1, T.pb1, lambda i: T.pd[:, 256 + i:257 + i], t1, i23, u1, s23,
                                                m23)):
        wait(V, (tk, 1), (ik, 1))
        for i in range(2):
            scan(e4(T.sf, 2 * h + i), e4(pa, i), off(i)).then_inc(sem[sk], 1)
        wait(V, (sk, 2), (uk, 1))
        tt(T.mk[:, 512 * h:512 * (h + 1)], T.sf[:, 512 * h:512 * (h + 1)], pb[:], op.is_gt).then_inc(sem[mk], 1)
    wait(P, (m01, 1))
    for i in range(2):
        P.matmul(T.pf[:, 0:256], T.idm[:], e4(T.mk, i), i == 0, False)
    wait(P, (ka[4], 1), (ka[5], 1))
    P.matmul(T.pc[:], T.ob[:], T.ao[:], True, True).then_inc(sem[tc], 1)
    wait(P, (m23, 1))
    for i in range(2, 4):
        m = P.matmul(T.pf[:, 0:256], T.idm[:], e4(T.mk, i), False, i == 3)
    m.then_inc(sem[opp], 1)
    wait(S, (opp, 1))
    S.activation(e4(T.ovl, ci), T.pf[:, 0:256], AF.Copy).then_inc(sem[ev], 1)
    wait(g, (ev, 1))
    send(tr(mates4, e4(T.ovl, ci), e4(T.ovl, ci), "ovs", low))

    wait(P, (s01, 2), (s23, 2), (sa[4], 1), (sa[5], 1))
    for x in range(2):
        P.matmul(sx(T.pd, x), T.kum[:], sl(T.ao, x), True, True).then_inc(sem[uc], 1)
    P.matmul(T.pd[:, 128:130], T.idf[:], F("cx"), True, False)
    P.matmul(T.pd[:, 128:130], T.lt[:], F("sm", 4, 2), False, True).then_inc(sem[uc], 1)
    P.matmul(T.pd[:, 130:132], T.al[:], F("sm", 4, 2), True, True).then_inc(sem[uc], 1)
    so2, c1k, qk, ek, f1, f2, f3, f4 = [ks() for _ in range(8)]
    lim = lambda x: -BIG + CAP * (x + 1)
    if isroot:
        vals()
    wait(V, (tc, 1), (uc, 4))
    for x in range(2):
        scan(e4(T.so, x), e4(T.pc, x), T.pd[:, 128 + x:129 + x]).then_inc(sem[so2], 1)
    for x in range(2):
        ts(c1("c1s", x), T.pd[:, 130 + x:131 + x], float(CAP), op.min, float(CAP * x), op.add).then_inc(sem[c1k], 1)
    wait(V, (so2, 2))
    for x in range(2):
        tt(sx(T.q1, x), sl(T.so, x), sx(T.pd, x), op.add).then_inc(sem[qk], 1)
    wait(V, (qk, 2))
    for x in range(2):
        ts(sx(T.qt, x), sx(T.q1, x), lim(x), op.is_gt, 2 * BIG, op.mult).then_inc(sem[f1], 1)
    wait(V, (f1, 2))
    tt(T.qe[:], T.q1[:], T.qt[:], op.add).then_inc(sem[f2], 1)
    wait(V, (f2, 1))
    tt(sx(T.mm, 2), sx(T.qe, 0), sx(T.qe, 1), op.min).then_inc(sem[f3], 1)
    wait(V, (f3, 1))
    tt(sx(T.mm, 3), sx(T.mm, 2), T.trs[:], op.min).then_inc(sem[f4], 1)
    wait(V, ("e2l", 16))
    for x in range(2):
        ts(e4(T.ee, x), e2w, float(2 * rk + x), op.is_equal).then_inc(sem[ek], 1)

    osk, u2k, s2k = [ks() for _ in range(3)]
    bk, sk2, tk2, ik2 = [[ks(), ks()] for _ in range(4)]
    f = [ks() for _ in range(7)]
    wait(P, (ev, 1))
    P.matmul(T.pf[:, 256:512], T.idm[:], e4(T.ovl, ci), True, False)
    wait(P, (so2, 2), (c1k, 2), (qk, 2))
    ini = (T.pc[:, 0:1], T.pd[:, 0:1])
    for x in range(2):
        P.matmul(ini[x], T.idf[:], c1("c1s", x), True, False)
    wait(P, ("ovs", 8 * (NC - 1)))
    oth = [c for c in range(NC) if c != ci]
    for c in oth:
        m = P.matmul(T.pf[:, 256:512], T.idm[:], e4(T.ovl, c), False, c == oth[-1])
    m.then_inc(sem[osk], 1)
    wait(V, (osk, 1), (ek, 2))
    for x in range(2):
        tt(e4(T.bb, x), e4(T.ee, x), T.pf[:, 256:512], op.min).then_inc(sem[bk[x]], 1)
    for x, pa in ((0, T.pa0), (1, T.pa1)):
        wait(S, (bk[x], 1))
        S.activation(e4(T.jk, 6 + x), e4(T.bb, x), AF.Copy, accum_out=c1("sm2", x)).then_inc(sem[sk2[x]], 1)
        wait(P, (bk[x], 1))
        P.matmul(pa[:, 0:256], T.ob[:], e4(T.bb, x), True, True).then_inc(sem[tk2[x]], 1)
        P.matmul(sx(T.pb0, x), T.kum[:], sl(T.bb, x), True, True).then_inc(sem[u2k], 1)
        wait(P, (sk2[x], 1))
        P.matmul(ini[x], T.lt[:], c1("sm2", x), False, True).then_inc(sem[ik2[x]], 1)
        wait(V, (tk2[x], 1), (ik2[x], 1))
        scan(e4(T.s2, x), pa[:, 0:256], ini[x]).then_inc(sem[s2k], 1)
    wait(V, (s2k, 2), (u2k, 2))
    for x in range(2):
        tt(sx(T.uu, x), sl(T.s2, x), sx(T.pb0, x), op.add).then_inc(sem[f[0]], 1)
    wait(V, (f[0], 2))
    for x in range(2):
        ts(sx(T.tt, x), sx(T.uu, x), lim(x), op.is_gt, 2 * BIG, op.mult).then_inc(sem[f[1]], 1)
    wait(V, (f[1], 2))
    tt(T.ef[:], T.uu[:], T.tt[:], op.add).then_inc(sem[f[2]], 1)
    wait(V, (f[2], 1))
    tt(sx(T.mm, 0), sx(T.ef, 0), sx(T.ef, 1), op.min).then_inc(sem[f[3]], 1)
    wait(V, (f[3], 1), (f4, 1))
    tt(sx(T.mm, 1), sx(T.mm, 0), sx(T.mm, 3), op.min).then_inc(sem[f[4]], 1)
    wait(V, (f[4], 1))
    ts(T.offs[:], sx(T.mm, 1), BIG - 1.0, op.add).then_inc(sem[f[5]], 1)
    wait(V, (f[5], 1))
    V.tensor_copy(T.win[:].indirect(T.offs[:]), T.val[:]).then_inc(sem[f[6]], 1)
    lk, lc = ks(), ks()
    wait(P, (f[6], 1))
    for b in range(NB):
        m = P.matmul(T.pb1[:, 2 * b:2 * b + 2], T.win[:, 128 * b:128 * (b + 1)], T.hl[:], True, True)
    m.then_inc(sem[lk], 1)
    wait(S, (lk, 1))
    S.activation(T.ls[:], T.pb1[:, 0:2 * NB], AF.Copy).then_inc(sem[lc], 1)
    if not isroot:
        wait(g, (lc, 1))
        send(tr([root], T.ls[:], T.lin[:, 2 * NB * (ci - 1):2 * NB * ci], "li%d" % ci, low))
        wait(g, ("loc", locn[0]))
        return

    r1, r2, r3, r4 = [ks() for _ in range(4)]
    wait(P, (lc, 1))
    P.matmul(T.pe[:, 0:2 * NB], T.idm[:], T.ls[:], True, False)
    for c in range(1, NC):
        wait(P, ("li%d" % c, 8))
        m = P.matmul(T.pe[:, 0:2 * NB], T.idm[:], T.lin[:, 2 * NB * (c - 1):2 * NB * c], False, c == NC - 1)
    m.then_inc(sem[r1], 1)
    wait(V, (r1, 1))
    V.tensor_copy(T.lsum[:], T.pe[:, 0:2 * NB]).then_inc(sem[r2], 1)
    wait(P, (r2, 1))
    for h in range(8):
        for i in range(2):
            m = P.matmul(T.pf[:, h:LQ:8], T.hsel[:, 128 * h:128 * (h + 1)], T.lsum[:, i:2 * NB:2], i == 0, i == 1)
    m.then_inc(sem[r3], 1)
    wait(V, (r3, 1))
    V.tensor_copy(T.lst[:], T.pf[:, 0:LQ]).then_inc(sem[r4], 1)
    CH, NCH = 40, LQ // 40
    xw = [("xl%d" % q, 16) for q in range(4)] + [("xland", nland), (r4, 1)]
    gk = [ks() for _ in range(NCH)]
    wait(V, *xw)
    wait(S, (fl, nfl), *xw)
    yc = lambda t, k: t[:, 16 * CH * k:16 * CH * (k + 1)]
    for k in range(NCH):
        w = T.land[:].indirect(T.lst[:, CH * k:CH * (k + 1)])
        if k % 2 == 0:
            V.tensor_copy(yc(T.ysb, k), w).then_inc(sem[gk[k]], 1)
        else:
            S.activation(yc(T.ysb, k), w, AF.Copy).then_inc(sem[gk[k]], 1)
    for k in range(NCH):
        q, s = (S, "ysc") if k == NCH - 1 else (Y, "yst")
        wait(q, (gk[k], 1))
        q.dma_start(yc(T.y, k), yc(T.ysb, k)).then_inc(sem[s], 16)
    wait(g, ("yst", 16 * (NCH - 1)), ("ysc", 16), ("loc", locn[0]))
